import numpy as np, ml_dtypes
CORES = [10,34,74,98]
N = 4
BF = ml_dtypes.bfloat16
def gentries(a):
    return np.ascontiguousarray(a.reshape(8, 16, -1).transpose(0, 2, 1)).reshape(8, -1)
def gtable(e):
    e = np.asarray(e); return np.ascontiguousarray(e.reshape(8, -1, 16).transpose(0, 2, 1)).reshape(128, -1).astype(np.int32)
L, B, V, W, DAYS, INTERVALS, H = 48, 64, 3072, 8192, 2, 3, 12
def parts(rng):
    x = rng.integers(28, 100, (N, 8, 1, V)) + rng.integers(-20, 21, (N, 8, 16, V))
    z = rng.integers(0, 65536, (N, 8, V))
    e = rng.integers(-75, 46, (8, 1, W)) + rng.integers(-20, 21, (8, 16, W))
    return x, z, e
def pack(x, z, e):
    x = np.minimum(np.maximum(x, 0), 127).reshape(N, 128, V); e = np.minimum(np.maximum(e, -128), 128).reshape(1, 128, W)
    return {"x": x.astype(np.float32).astype(BF), "boat": np.stack([gtable(a) for a in z]), "enc": np.repeat(e, N, axis=0).astype(np.float32).astype(BF)}
def timed(rng, z, g):
    r = rng.integers(0, W); z[:, g] = r + W * rng.integers(0, 65536 // W, (N, V))
    return (138 * r + 811 * np.arange(DAYS * INTERVALS + DAYS)) % W
def setup_inputs(rng):
    return pack(*parts(rng))
def setup_inputs_ties(rng):
    x, z, e = parts(rng)
    x = rng.integers(20, 100, (1, 8, 16, 1)) + rng.integers(0, 2, (N, 8, 1, V))
    n = rng.choice(np.array([0, H - 1, H - 1, H, H, H + 1, 16]), (8, 1, W)); up = np.argsort(rng.random((8, 16, W)), axis=1) < n
    e = rng.choice(np.array([0, 0, 1, 1, 1, 2]), (8, 1, W)) - 1 + up
    return pack(x, z, e)
def setup_inputs_order(rng):
    x, z, e = parts(rng); b = np.arange(B); k = INTERVALS; q = b % (2 * k)
    st = np.stack([127 - 2 * b, 1 + 2 * b, np.where(q < k, 10 * (k - q), 10 * (3 * k - q)), 64 + 0 * b, np.where(b == 0, 120, np.where(b == B - 1, 127, 1 + 2 * b))])
    kind = rng.integers(0, 6, (N, 8, L)); kind[:, :, :6] = np.arange(6); kind[:, :, L - 6:] = rng.permutation(6)
    s = st[np.minimum(kind, 4)].transpose(0, 1, 3, 2).reshape(N, 8, 1, V)
    x = np.where(np.tile(kind == 5, (1, 1, B))[:, :, None, :], x, s)
    e = np.where(rng.random((8, 16, W)) < rng.random((8, 1, W)), 1, rng.integers(-1, 1, (8, 16, W)))
    return pack(x, z, e)
def setup_inputs_alike(rng):
    x, z, e = parts(rng); zz = z.reshape(N, 8, B, L).copy(); inv = pow(37, -1, W)
    for b in range(1, B):
        c = rng.choice(np.array([0, W - 1]), (N, 8, L))
        zz[:, :, b] = (c - 101 * zz[:, :, b - 1]) % W * inv % W + W * rng.integers(0, 65536 // W, (N, 8, L))
    zz[:, :, :, 1::2] = rng.choice(np.array([0, 65535, 65535, 1]), (N, 8, B, len(range(1, L, 2))))
    e[:, :, 0] = rng.integers(-10, 31, (8, 16)); e[:, :, W - 1] = rng.integers(-30, 11, (8, 16))
    g = rng.permutation(8); odd = np.arange(N)[:, None, None] % 2 == 1
    for i, (c, s) in enumerate(((0, 1), (W - 1, -1))):
        a = rng.integers(0, W, L); b = (c - 811 * DAYS * INTERVALS - 101 * a) % W * inv % W
        zz[:, g[i]] = np.where(odd, b, a) + W * rng.integers(0, 65536 // W, (N, B, L))
        e[g[i]][:, c] = s * rng.integers(112, 129, 16); e[g[i]][:, c + s] = -s * rng.integers(112, 129, 16)
    return pack(x, zz.reshape(N, 8, V), e)
def setup_inputs_flat(rng):
    x, z, e = parts(rng); g = rng.permutation(8); k = INTERVALS; last = (DAYS - 1) * k
    e[g[0]] = -128; e[g[1]] = 128
    x[:, g[1]] = np.where(rng.random((N, 1, V)) < 0.5, x[:, g[1]], 127 * rng.integers(0, 2, (N, 1, V)))
    e[g[2]] = 127; x[:, g[2]] = 127 * rng.integers(0, 2, (N, 16, V))
    e[g[3]] = rng.choice(np.array([-127, -126]), (1, W)); x[:, g[3]] = 127 * rng.integers(0, 2, (N, 1, V))
    c = timed(rng, z, g[4]); e[g[4]][:, c[:k - 1]] = -128; e[g[4]][:, c[k - 1]] = 128
    c = timed(rng, z, g[5]); e[g[5]][:, c[last]] = -128; e[g[5]][:, c[last + 1]] = rng.integers(127, 129, 16)
    c = timed(rng, z, g[6]); e[g[6]][:, c[:-1]] = -128; e[g[6]][:, c[[last, last + k - 1]]] = 0
    b = np.arange(B)[:, None]; s = np.where(b == 0, 120, np.where(b == B - 1, 127, 1 + 2 * b))
    x[:, g[6]] = np.where(rng.random((N, 1, 1, L)) < 0.5, s, x[:, g[6]].reshape(N, 16, B, L)).reshape(N, 16, V)
    return pack(x, z, e)
def setup_inputs_spread(rng):
    x = np.floor(127.99 * np.exp2(-6 * rng.random((N, 8, 1, V))) * rng.random((N, 8, 16, V))).astype(np.int64)
    z = np.minimum(np.exp2(16 * rng.random((N, 8, V))).astype(np.int64), 65535) - 1 + rng.integers(0, 2, (N, 8, V))
    e = np.rint(128 * np.exp2(-7 * rng.random((8, 1, W))) * (0.25 + 0.75 * rng.random((8, 16, W)))).astype(np.int64) * (2 * rng.integers(0, 2, (8, 1, W)) - 1)
    return pack(x, z, e)
def check_inputs(d):
    bad = []
    for k, lo, hi in (("x", 0, 127), ("boat", 0, 65535), ("enc", -128, 128)):
        v = np.asarray(d[k]).astype(np.float32)
        if not np.all((v >= lo) & (v <= hi) & (v == np.floor(v))): bad.append("range of " + k)
    v = np.asarray(d["enc"]).astype(np.float32)
    if not np.all(v == v[:1]): bad.append("enc alike on all ranks")
    return bad
def beats(xi, zi, xj, zj, e, t):
    c = (37 * zi + 101 * zj + 811 * t) & (W - 1)
    v = np.take_along_axis(e, c[:, :, None, :], 3)
    return np.add.reduce((xi + v > xj).astype(np.int64), axis=2) >= H
def reference(x, boat, enc):
    X = x.astype(np.float32).reshape(N, 8, 16, V); E = enc.astype(np.float32).reshape(N, 8, 16, W)
    Z = np.stack([gentries(a) for a in boat]).astype(np.int64)
    for day in range(DAYS):
        rowing = np.ones((N, 8, V), bool); place = np.tile(np.arange(V), (N, 8, 1))
        for k in range(INTERVALS):
            row = rowing.reshape(N, 8, B, L); rival = np.full((N, 8, B, L), -1); last = np.full((N, 8, L), -1)
            for b in range(B):
                rival[:, :, b] = np.where(row[:, :, b], last, -1)
                last = np.where(row[:, :, b], b * L + np.arange(L), last)
            rival = rival.reshape(N, 8, V); j = np.maximum(rival, 0)
            w = beats(X, Z, np.take_along_axis(X, j[:, :, None, :], 3), np.take_along_axis(Z, j, 2), E, day * INTERVALS + k) & (rival >= 0)
            w = w.reshape(N, 8, B, L); bump = np.zeros((N, 8, B, L), bool); before = np.zeros((N, 8, L), bool)
            for b in range(B):
                bump[:, :, b] = w[:, :, b] & ~before
                before = np.where(row[:, :, b], bump[:, :, b], before)
            i0, i1, i2 = np.nonzero(bump.reshape(N, 8, V)); jj = j[i0, i1, i2]
            place[i0, i1, i2] = jj; place[i0, i1, jj] = i2
            rowing[i0, i1, i2] = False; rowing[i0, i1, jj] = False
        X = np.take_along_axis(X, place[:, :, None, :], 3); Z = np.take_along_axis(Z, place, 2)
        hx, hz = np.array(X[1:, :, :, :L]), np.array(Z[1:, :, :L]); fx, fz = np.array(X[:-1, :, :, V - L:]), np.array(Z[:-1, :, V - L:])
        w = beats(hx, hz, fx, fz, E[1:], DAYS * INTERVALS + day); wx = w[:, :, None, :]
        X[1:, :, :, :L] = np.where(wx, fx, hx); Z[1:, :, :L] = np.where(w, fz, hz)
        X[:-1, :, :, V - L:] = np.where(wx, hx, fx); Z[:-1, :, V - L:] = np.where(w, hz, fz)
    return {"yx": X.reshape(N, 128, V).astype(BF), "yb": np.stack([gtable(a) for a in Z]).astype(np.float32)}

@@ -1,0 +1,537 @@
+from concourse.bass import DstId, RemoteDMATransfer
+from concourse.mybir import AluOpType, ActivationFunctionType
+
+A = AluOpType
+ACT = ActivationFunctionType
+AND, SHR = A.bitwise_and, A.logical_shift_right
+C = float(2 ** 25)
+HUGE = float(2 ** 60)
+CW = 1040
+NV = 30
+NA = 18
+
+
+def centred(v):
+    v %= 8192
+    return v - 8192 if v >= 4096 else v
+
+
+INV = centred(pow(101, -1, 8192))
+BETA = centred(37 * INV)
+
+F, H, I, U = "float32", "bfloat16", "int32", "uint16"
+SCRATCH = {}
+for _n, _w, _t in (("xn", 3072, H), ("outb", 3072, H), ("ew", 8192, H), ("bt", 192, I), ("xa", 3 * CW, H), ("xb", 3 * CW, H), ("sel", 2048, H),
+                   ("jb0", 128, H), ("jb1", 128, H), ("jb", 128, H), ("one", 128, H), ("idp", 128, H), ("idn", 128, H), ("blk", 128, H),
+                   ("kc", 64, H), ("kcb", 64, H), ("pi", 1, I), ("pj", 1, I), ("sv", 8, F), ("io48", 64, I), ("iob", 64, I),
+                   ("pos", 64, F), ("zero", 64, F), ("neg", 64, H), ("rl", 192, U), ("n1", 192, I), ("n2", 192, I), ("n3", 192, I),
+                   ("wf", 192, I), ("ni", 192, I), ("so", 192, I), ("su", 192, U), ("h1", 6, I), ("h2", 6, I), ("h3", 6, I), ("hu", 6, U), ("hw", 6, I),
+                   ("q1", 6, I), ("q2", 6, I), ("bu", 12, U), ("mc", 96, F), ("mm", 96, F), ("mcmp", 96, H), ("mw", 96, F), ("fin", 96, H),
+                   ("nd", 6, F), ("nw", 6, F), ("nm", 6, F), ("pn", 12, F), ("p1", 12, I), ("p2", 12, I), ("p3", 12, I), ("yn", 192, F), ("db", 96, H),
+                   ("tx0", 108, F), ("tx1", 108, F), ("rx0", 108, F), ("rx1", 108, F), ("xo", 3 * 16 * NV, H)):
+    SCRATCH[_n] = ("sbuf", [128, _w], _t)
+for _c in range(3):
+    for _n, _w, _t in (("s", 64, F), ("x", 64, F), ("t", 64, F), ("nm", 64, F), ("ys", 64, F), ("ra", 64, F), ("rb", 64, F), ("ma", 64, H), ("mb", 64, H),
+                       ("sg", 64, H), ("cs", 64, I), ("ca", 64, I), ("oi", 64, I), ("cu", 64, U), ("of", 64, U),
+                       ("dv", 1008, H), ("cmp", 1008, H), ("xr", 1008, H), ("es", 1008, H)):
+        SCRATCH["%s_%d" % (_n, _c)] = ("sbuf", [128, _w], _t)
+PSUM = ("va", "vb", "z0", "z1", "z2", "u0", "u1", "u2")
+for _n in PSUM:
+    SCRATCH[_n] = ("psum", [128, 512], F)
+QSEM = {"v": "qv", "s": "qs", "p": "qp", "g": "qg"}
+SEMAPHORES = ["qv", "qs", "qp", "qg", "db", "dx", "de", "o1", "o2", "o3", "o4", "o5", "rh0", "rf0", "rh1", "rf1", "loc"]
+
+
+def B(name, a, b, step=1):
+    return (name, a, b, step)
+
+
+def IND(w, o):
+    return ("ind", w, o)
+
+
+def entries(v):
+    return entries(v[1]) + entries(v[2]) if v[0] == "ind" else [v[:3]]
+
+
+def own(x, c, j0, j1, shift=0):
+    a = c * CW + 16 * (j0 + 2 + shift)
+    return B(x, a, a + 16 * (j1 - j0))
+
+
+def win(x, c):
+    return B(x, c * CW, (c + 1) * CW)
+
+
+def Y(c, a=0, b=64):
+    return B("va", 64 * c + a, 64 * c + b)
+
+
+def ACC(c):
+    return B("va", 192 + 64 * c, 256 + 64 * c)
+
+
+NBX, NBR = B("va", 385, 449), B("va", 384, 448, -1)
+
+
+def UT(c, a=0, b=64):
+    return B("vb", 64 * c + a, 64 * c + b)
+
+
+def VT(c, step=1):
+    return B("vb", 192 + 64 * c, 256 + 64 * c, step)
+
+
+def t_(n, c, a=0, b=64, step=1):
+    return B("%s_%d" % (n, c), a, b, step)
+
+
+def R(c, k, a=0, b=64):
+    return t_("rb" if k % 2 else "ra", c, a, b)
+
+
+def M(c, k, step=1):
+    return t_("mb" if k % 2 else "ma", c, 0, 64, step)
+
+
+EW = B("ew", 0, 8192)
+IDP, IDN = B("idp", 0, 128), B("idn", 0, 128)
+
+
+def rank_program(g, core, T, topo):
+    rank = T.rank_of(core)
+    if rank is None:
+        return
+    n_ranks = len(T.cores)
+    up, down = rank > 0, rank < n_ranks - 1
+    queue = {"v": g.vector, "s": g.scalar, "p": g.tensor, "g": g, "y": g.sync}
+    count = {}
+    waited = {}
+    log = {}
+
+    def need(q, sem, val):
+        if waited.get((q, sem), 0) < val:
+            waited[(q, sem)] = val
+            queue[q].wait_ge(T.sem[sem], val)
+
+    def ap(v):
+        if v[0] == "ind":
+            return ap(v[1]).indirect(ap(v[2]))
+        name, a, b, step = v
+        if step == -1:
+            return T[name][:, b - 1:(a - 1 if a > 0 else None):-1]
+        return T[name][:, a:b] if step == 1 else T[name][:, a:b:step]
+
+    def sync(q, reads, writes, sem, n):
+        waits, new = {}, []
+        for kind, views in (("r", reads), ("w", writes)):
+            for v in views:
+                for name, a, b in entries(v):
+                    ps = name in PSUM
+                    for k2, a2, b2, q2, s2, v2 in log.get(name, []):
+                        if not ((ps and q2 != q) or (a < b2 and a2 < b and not (kind == "r" and k2 == "r"))):
+                            continue
+                        if q2 == q == "p":
+                            continue
+                        waits[s2] = max(waits.get(s2, 0), v2)
+                    new.append((name, kind, a, b))
+        for s2 in sorted(waits):
+            need(q, s2, waits[s2])
+        count[sem] = count.get(sem, 0) + n
+        for name, kind, a, b in new:
+            old = log.setdefault(name, [])
+            if kind == "w":
+                old[:] = [e for e in old if not (a <= e[1] and e[2] <= b and (name not in PSUM or e[3] == q))]
+            else:
+                old[:] = [e for e in old if not (e[0] == "r" and e[3] == q and a <= e[1] and e[2] <= b)]
+            old.append((kind, a, b, q, sem, count[sem]))
+
+    def op(q, reads, writes, call):
+        sync(q, reads, writes, QSEM[q], 1)
+        call().then_inc(T.sem[QSEM[q]], 1)
+
+    def tt(out, a, b, o):
+        op("v", [a, b], [out], lambda: g.vector.tensor_tensor(ap(out), ap(a), ap(b), o))
+
+    def ts(out, a, s1, o1, s2=None, o2=None):
+        rd = [a] + ([s1] if isinstance(s1, tuple) else [])
+        p1 = ap(s1) if isinstance(s1, tuple) else s1
+        if o2 is None:
+            op("v", rd, [out], lambda: g.vector.tensor_scalar(ap(out), ap(a), p1, None, o1))
+        else:
+            op("v", rd, [out], lambda: g.vector.tensor_scalar(ap(out), ap(a), p1, s2, o1, o2))
+
+    def cp(out, a):
+        op("v", [a], [out], lambda: g.vector.tensor_copy(ap(out), ap(a)))
+
+    def scan(out, d0, d1, init, o0, o1):
+        op("v", [d0, d1], [out], lambda: g.vector.tensor_tensor_scan(ap(out), ap(d0), ap(d1), init, o0, o1))
+
+    def fill(out, val):
+        op("v", [], [out], lambda: g.vector.memset(ap(out), val))
+
+    def act(out, a, func, **kw):
+        op("s", [a], [out], lambda: g.scalar.activation(ap(out), ap(a), func, **kw))
+
+    def mm(out, lhs, rhs, start, stop):
+        op("p", [lhs, rhs], [out], lambda: g.tensor.matmul(ap(out), ap(lhs), ap(rhs), start, stop))
+
+    def dma(q, out, a, sem, out_ap=None, in_ap=None):
+        sync(q, [a] if a else [], [out] if out else [], sem, 16)
+        queue[q].dma_start(ap(out) if out else out_ap, ap(a) if a else in_ap).then_inc(T.sem[sem], 16)
+
+    def gi(out, pattern, base, cm, **kw):
+        op("g", [], [out], lambda: g.iota(ap(out), pattern, base, cm, **kw))
+
+    def gsel(out, a, pattern, cmpop, val, base, cm):
+        op("g", [a], [out], lambda: g.affine_select(ap(out), ap(a), pattern, cmpop, val, base, cm))
+
+    dma("y", B("bt", 0, 192), None, "db", in_ap=T.boat[:])
+    dma("s", B("xn", 0, 3072), None, "dx", in_ap=T.x[:])
+    dma("y", EW, None, "de", in_ap=T.enc[:])
+
+    gi(B("pi", 0, 1), [[0, 1]], 0, 1)
+    gi(B("io48", 0, 64), [[48, 64]], 0, 0)
+    gi(B("iob", 0, 64), [[1, 64]], 1, 0)
+    gi(B("jb0", 0, 128), [[0, 8], [1, 16]], 0, 0, allow_small_or_imprecise_dtypes=True)
+    fill(B("one", 0, 128), 1.0)
+    gsel(B("jb1", 0, 128), B("jb0", 0, 128), [[-16, 8], [0, 16]], A.is_ge, -1.0, 0, 1)
+    gsel(B("jb", 0, 128), B("jb1", 0, 128), [[16, 8], [0, 16]], A.is_ge, -1.0, 15, -1)
+    gsel(IDP, B("one", 0, 128), [[-1, 128]], A.is_equal, 0.0, 0, 1)
+    fill(B("zero", 0, 64), 0.0)
+    fill(B("neg", 0, 64), -1.0)
+    for c in range(3):
+        fill(B("xa", c * CW, c * CW + 16), 512.0)
+        fill(B("xb", c * CW, c * CW + 16), 512.0)
+    for k in ("kc", "kcb"):
+        fill(B(k, 0, 64), -7.0 * C)
+        fill(B(k, 1, 1 + NV), -11.5 * C)
+        fill(B(k, 0, 1), -float(2 ** 30))
+    fill(B("kcb", 63, 64), -11.5 * C)
+    fill(B("va", 448, 449), 0.0)
+    ts(B("pj", 0, 1), B("pi", 0, 1), 15, AND)
+    for c in range(3):
+        ts(B("sv", c, c + 1), B("pj", 0, 1), float(CW * c), A.add)
+        ts(B("sv", 4 + c, 5 + c), B("pj", 0, 1), float(16 * c), A.add)
+    for c in range(3):
+        ts(B("rl", 64 * c, 64 * c + 64), B("io48", 0, 64), B("sv", 4 + c, 5 + c), A.add)
+    ts(B("pos", 0, 64), B("iob", 0, 64), 131072.0, A.mult)
+
+    def move(q, dst, src):
+        if q == "v":
+            cp(dst, src)
+        else:
+            act(dst, src, ACT.Copy)
+
+    def relay(q, c, b0, b1):
+        move(q, own("xa", c, b0 - 1, b1 - 1), IND(B("xn", 0, 3072), B("rl", 64 * c + b0, 64 * c + b1)))
+
+    def perm(q, c, b0, b1):
+        move(q, own("xb", c, b0 - 1, b1 - 1), IND(win("xa", c), B("su", 64 * c + b0, 64 * c + b1)))
+
+    def xo(c):
+        return B("xo", 16 * NV * c, 16 * NV * (c + 1))
+
+    def place_words(c, a=0, b=64):
+        tt(Y(c, a, b), B("wf", 64 * c + a, 64 * c + b), B("pos", a, b), A.add)
+        e = min(b, 63)
+        if e > a:
+            cp(R(c, 0, a + 1, e + 1), Y(c, a, e))
+
+    def first_list(c):
+        tt(t_("cs", c, 0, 63), UT(c, 1, 64), B("wf", 64 * c, 64 * c + 63), A.add)
+        ts(t_("ca", c, 0, 63), t_("cs", c, 0, 63), 8191, AND)
+        cp(t_("cu", c, 0, 63), t_("ca", c, 0, 63))
+
+    turn = [0]
+
+    def bank():
+        turn[0] += 1
+        return "u%d" % (turn[0] % 3)
+
+    def first_diff(x, c):
+        o = B(bank(), 0, 16 * NV)
+        mm(o, IDP, own(x, c, 0, NV, -1), True, False)
+        mm(o, IDN, own(x, c, 0, NV), False, True)
+        act(t_("dv", c, 0, 16 * NV), o, ACT.Copy)
+
+    def race_v_diff(x, c):
+        tt(t_("dv", c, 0, 16 * NV), IND(win(x, c), t_("of", c, 0, NV)), xo(c), A.subtract)
+
+    def race_v(c):
+        tt(t_("cmp", c, 0, 16 * NV), IND(EW, t_("cu", c, 0, NV)), t_("dv", c, 0, 16 * NV), A.is_gt)
+
+    def race_s(x, c, k):
+        halves = ((bank(), NV, NV + NA), (bank(), NV + NA, 63))
+        if k:
+            act(t_("xr", c, 16 * NV, 1008), IND(win(x, c), t_("of", c, NV, 63)), ACT.Copy)
+        for p, j0, j1 in halves:
+            o = B(p, 0, 16 * (j1 - j0))
+            mm(o, IDP, own(x, c, j0, j1), True, False)
+            mm(o, IDN, t_("xr", c, 16 * j0, 16 * j1) if k else own(x, c, j0, j1, -1), False, False)
+            act(t_("es", c, 16 * j0, 16 * j1), IND(EW, t_("cu", c, j0, j1)), ACT.Copy)
+            mm(o, IDP, t_("es", c, 16 * j0, 16 * j1), False, True)
+        for p, j0, j1 in halves:
+            act(t_("cmp", c, 16 * j0, 16 * j1), B(p, 0, 16 * (j1 - j0)), ACT.Sign, bias=-0.5)
+
+    def counts(c, k, kc="kc"):
+        z = "z%d" % c
+        mm(B(z, 0, 64), IDP, B(kc, 0, 64), True, False)
+        if k:
+            mm(B(z, 0, 64), IDP, M(c, k), False, False)
+        for s in range(16):
+            mm(B(z, 1, 64), B("sel", 128 * s, 128 * s + 128), t_("cmp", c, s, 1008, 16), False, s == 15)
+
+    def post(c, k):
+        last = k == 2
+        scan(t_("s", c), t_("sg", c) if k else B("neg", 0, 64), B("z%d" % c, 0, 64), -1.0, A.mult, A.min)
+        tt(VT(c), Y(c), t_("s", c), A.min)
+        scan(NBR, M(c, k, -1) if k else B("zero", 0, 64, -1), VT(c, -1), 0.0, A.min, A.max)
+        tt(t_("t", c), VT(c), R(c, k), A.min)
+        tt(t_("x", c), t_("s", c), NBX, A.max)
+        if k:
+            tt(t_("nm", c), NBX, M(c, k), A.subtract)
+        else:
+            tt(ACC(c), NBX, t_("t", c), A.max)
+        tt(t_("ys", c) if last else Y(c), Y(c), t_("x", c), A.subtract)
+        if k:
+            tt(ACC(c), ACC(c), t_("t", c), A.max)
+        if not last:
+            scan(R(c, k + 1, 1, 64), Y(c, 0, 63), B("zero", 0, 63), 0.0, A.max, A.max)
+        if k:
+            tt(ACC(c), ACC(c), t_("nm", c), A.max)
+        if last:
+            tt(ACC(c), ACC(c), t_("ys", c), A.max)
+            return
+        tt(t_("cs", c, 0, 63), UT(c, 1, 64), R(c, k + 1, 1, 64), A.add)
+        ts(M(c, k + 1), Y(c), 0.0, A.is_le, HUGE, A.mult)
+        ts(t_("oi", c, 0, 63), t_("cs", c, 0, 63), 13, SHR, 0x7F0, AND)
+        ts(t_("ca", c, 0, 63), t_("cs", c, 0, 63), 8191, AND)
+        ts(t_("of", c, 0, 63), t_("oi", c, 0, 63), B("sv", 0, 1), A.add)
+        cp(t_("cu", c, 0, 63), t_("ca", c, 0, 63))
+
+    def later_intervals(x):
+        for k in range(2):
+            for c in range(3):
+                post(c, k)
+                race_v_diff(x, c)
+                ts(t_("sg", c), M(c, k + 1), 2.0 / HUGE, A.mult, -1.0, A.add)
+                if k == 0:
+                    ts(UT(c), UT(c), 811.0, A.add)
+                race_v(c)
+                race_s(x, c, k + 1)
+                counts(c, k + 1)
+
+    TS, TW, TU = (6, 54), (0, 102), (3, 105)
+    RS, RW, RU = (0, 60), (48, 54), (51, 57)
+
+    def heads_and_feet(day, x):
+        tx = "tx%d" % day
+        h1, h2, h3, hw = B("h1", 0, 6), B("h2", 0, 6), B("h3", 0, 6), B("hw", 0, 6)
+        cp(B("h1", 0, 3), B("va", 192, 384, 64))
+        cp(B("h1", 3, 6), B("va", 192 + 63, 384, 64))
+        ts(h2, h1, 13, SHR, 0x7F0, AND)
+        ts(hw, h1, 65535, AND)
+        for c in range(3):
+            ts(B("hu", c, 6, 3), B("h2", c, 6, 3), B("sv", c, c + 1), A.add)
+        ts(h3, h1, 8191, AND)
+        cp(B(tx, 6, 102), IND(B(x, 0, 3 * CW), B("hu", 0, 6)))
+        ts(h1, h3, -4096.0, A.add, float(BETA), A.mult)
+        for i in range(2):
+            cp(B(tx, TW[i], TW[i] + 3), B("hw", 3 * i, 3 * i + 3))
+        ts(h3, h1, 8191, AND)
+        for i in range(2):
+            cp(B(tx, TU[i], TU[i] + 3), B("h3", 3 * i, 3 * i + 3))
+
+    def send(day):
+        tx, rx = "tx%d" % day, "rx%d" % day
+        calls = ([(rank - 1, 0, 54, "rh%d" % day)] if up else []) + ([(rank + 1, 54, 0, "rf%d" % day)] if down else [])
+        sync("g", [B(tx, 0, 108)], [], "loc", 0)
+        trs = []
+        for i, (r, a, b, sem) in enumerate(calls):
+            es = topo.engines(core, T.cores[r])
+            es = es[i * len(es) // len(calls):(i + 1) * len(es) // len(calls)]
+            rid, pid, _ = topo.addr(T.cores[r])
+            trs.append(RemoteDMATransfer(dst_ids=[DstId(rid=rid, pnc=pid)], dma_engine_mask=sum(1 << e for e in es), remote_sem=T.sem[sem],
+                                         src=T[tx][:, a:a + 54], dst=T[rx][:, b:b + 54]))
+            count["loc"] = count.get("loc", 0) + len(es)
+        g.remote_dma_fused(trs, local_sem=T.sem["loc"])
+        for ok, r, a, sem in ((up, rank - 1, 0, "rf%d" % day), (down, rank + 1, 54, "rh%d" % day)):
+            if ok:
+                fan = (1 if r > 0 else 0) + (1 if r < n_ranks - 1 else 0)
+                count[sem] = len(topo.engines(T.cores[r], core)) // fan
+                log.setdefault(rx, []).append(("w", a, a + 54, "remote", sem, count[sem]))
+
+    parts = [i for i, ok in ((0, up), (1, down)) if ok]
+    lo, hi = 48 * parts[0], 48 * parts[-1] + 48
+    la, lb = lo // 16, hi // 16
+
+    def decode(n0, n1):
+        p1, p2, p3 = B("p1", n0, n1), B("p2", n0, n1), B("p3", n0, n1)
+        ts(p2, p1, 8191, AND)
+        ts(p3, p1, 57344, AND)
+        ts(p1, p2, -4096.0, A.add, float(INV), A.mult)
+        ts(p2, p1, 4096.0, A.add)
+        ts(p1, p2, 8191, AND)
+        tt(B("pn", n0, n1), p1, p3, A.add)
+
+    def meeting(day):
+        tx, rx = "tx%d" % day, "rx%d" % day
+        for i in parts:
+            hd, ft = (tx, rx) if i == 0 else (rx, tx)
+            u, w = (TU if i == 0 else RU)[i], (RW if i == 0 else TW)[i]
+            tt(B("nm", 3 * i, 3 * i + 3), B(hd, u, u + 3), B(ft, w, w + 3), A.add)
+        ts(B("q1", la, lb), B("nm", la, lb), float(4096 + 811 * (6 + day)), A.add)
+        for i in parts:
+            o, r = B(tx, TS[i], TS[i] + 48), B(rx, RS[i], RS[i] + 48)
+            tt(B("mc", 48 * i, 48 * i + 48), o if i else r, r if i else o, A.subtract)
+        ts(B("q2", la, lb), B("q1", la, lb), 8191, AND)
+        cp(B("hu", 0, lb - la), B("q2", la, lb))
+        tt(B("mcmp", lo, hi), IND(EW, B("hu", 0, lb - la)), B("mc", lo, hi), A.is_gt)
+        mm(B("z0", lo, hi), B("blk", 0, 128), B("mcmp", lo, hi), True, True)
+        for s in range(16):
+            mm(B("z1", la, lb), B("sel", 128 * s, 128 * s + 128), B("mcmp", lo + s, hi, 16), s == 0, s == 15)
+        if day:
+            for i in parts:
+                cp(B("p1", 6 * i, 6 * i + 3), B(tx, TW[i], TW[i] + 3))
+                cp(B("p1", 6 * i + 3, 6 * i + 6), B(rx, RW[i], RW[i] + 3))
+            decode(6 * parts[0], 6 * parts[-1] + 6)
+        src = []
+        for i in parts:
+            o = B("pn", 6 * i, 6 * i + 3) if day else B(tx, TW[i], TW[i] + 3)
+            r = B("pn", 6 * i + 3, 6 * i + 6) if day else B(rx, RW[i], RW[i] + 3)
+            tt(B("nd", 3 * i, 3 * i + 3), r, o, A.subtract)
+            src.append((i, o))
+        ts(B("mw", lo, hi), B("z0", lo, hi), 11.5, A.is_gt)
+        ts(B("nw", la, lb), B("z1", la, lb), 11.5 * C, A.is_gt)
+        tt(B("mm", lo, hi), B("mw", lo, hi), B("mc", lo, hi), A.mult)
+        tt(B("nm", la, lb), B("nw", la, lb), B("nd", la, lb), A.mult)
+        return src
+
+    n1, n2, n3 = B("n1", 0, 192), B("n2", 0, 192), B("n3", 0, 192)
+    ni, wf, ut = B("ni", 0, 192), B("wf", 0, 192), B("vb", 0, 192)
+    for c in range(3):
+        cp(B("n1", 64 * c, 64 * c + 64), B("bt", c, 192, 3))
+    ts(n2, n1, 101.0, A.mult)
+    ts(n3, n1, 57344, AND)
+    ts(ni, n2, 8191, AND)
+    ts(n2, n1, 37.0, A.mult)
+    tt(wf, ni, n3, A.add)
+    ts(n3, n2, 8191, AND)
+    cp(ut, n3)
+    for c in range(3):
+        place_words(c)
+        fill(R(c, 0, 0, 1), 0.0)
+        fill(R(c, 1, 0, 1), 0.0)
+        first_list(c)
+        ts(UT(c), UT(c), 811.0, A.add)
+    relay("s", 0, 0, 64)
+    relay("v", 1, 0, 64)
+    relay("s", 2, 0, 32)
+    relay("v", 2, 32, 64)
+    ts(IDN, IDP, -1.0, A.mult)
+    ts(B("blk", 0, 128), B("jb", 0, 128), 0.0, A.is_ge)
+    for s in range(16):
+        ts(B("sel", 128 * s, 128 * s + 128), B("jb", 0, 128), float(s), A.is_equal, C, A.mult)
+    for c in range(3):
+        first_diff("xa", c)
+        cp(xo(c), own("xa", c, 0, NV))
+    for c in range(3):
+        race_v(c)
+        race_s("xa", c, 0)
+        counts(c, 0)
+    later_intervals("xa")
+
+    def source(c):
+        sl = (64 * c, 64 * c + 64)
+        cp(B("ni", *sl), ACC(c))
+        ts(B("so", *sl), B("ni", *sl), 13, SHR, 0x7F0, AND)
+
+    def source_list(c):
+        source(c)
+        ts(B("su", 64 * c, 64 * c + 64), B("so", 64 * c, 64 * c + 64), B("sv", 0, 1), A.add)
+    for c in range(3):
+        post(c, 2)
+        if c < 2:
+            source_list(c)
+            perm("s", c, 0, 64)
+    heads_and_feet(0, "xa")
+    send(0)
+    source_list(2)
+    perm("s", 2, 32, 64)
+    perm("v", 2, 0, 32)
+
+    ts(n2, ni, 8191, AND)
+    ts(wf, ni, 65535, AND)
+    ts(n3, n2, -4096.0, A.add, float(BETA), A.mult)
+    ts(n2, n3, 8191, AND)
+    ts(ut, n2, float(4096 + 811 * 3), A.add)
+    for c in range(3):
+        first_diff("xb", c)
+    for c in range(3):
+        first_list(c)
+        race_s("xb", c, 0)
+    for c in range(3):
+        race_v(c)
+    for c in range(3):
+        place_words(c)
+        cp(xo(c), own("xb", c, 0, NV))
+    for i, o in meeting(0):
+        for c in range(3):
+            tt(own("xb", c, 63 * i - 1, 63 * i), B("tx0", TS[i] + 16 * c, TS[i] + 16 * c + 16), B("mm", 48 * i + 16 * c, 48 * i + 16 * c + 16), A.subtract if i else A.add)
+        tt(B("wf", 63 * i, 192, 64), o, B("nm", 3 * i, 3 * i + 3), A.add)
+    if down:
+        ts(B("h2", 0, 3), B("wf", 63, 192, 64), 8191, AND)
+        ts(B("h1", 0, 3), B("h2", 0, 3), -4096.0, A.add, float(BETA), A.mult)
+        ts(B("h2", 0, 3), B("h1", 0, 3), 8191, AND)
+        ts(B("vb", 63, 192, 64), B("h2", 0, 3), float(4096 + 811 * 3), A.add)
+    tt(B("q1", 0, 3), B("vb", 1, 192, 64), B("wf", 0, 192, 64), A.add)
+    tt(B("q1", 3, 6), B("vb", 63, 192, 64), B("wf", 62, 192, 64), A.add)
+    ts(B("q2", 0, 6), B("q1", 0, 6), 8191, AND)
+    cp(B("bu", 0, 12, 2), B("q2", 0, 6))
+    ends = [(c, j, 16 * (c + i), 2 * (c + i)) for c in range(3) for i, j in ((0, 0), (3, 62))]
+    for c, j, a, l in ends:
+        tt(B("db", a, a + 16), own("xb", c, j, j + 1, -1), own("xb", c, j, j + 1), A.subtract)
+    for c, j, a, l in ends:
+        tt(t_("cmp", c, 16 * j, 16 * j + 16), IND(EW, B("bu", l, l + 1)), B("db", a, a + 16), A.is_gt)
+        if j:
+            counts(c, 0, "kcb")
+    for c in range(3):
+        place_words(c, 0, 1)
+        place_words(c, 63, 64)
+        ts(UT(c), UT(c), 811.0, A.add)
+    later_intervals("xb")
+
+    def final_source(c):
+        source(c)
+        ts(B("su", c, 192, 3), B("so", 64 * c, 64 * c + 64), B("sv", c, c + 1), A.add)
+    for c in range(3):
+        post(c, 2)
+        if c < 2:
+            final_source(c)
+    heads_and_feet(1, "xb")
+    send(1)
+    final_source(2)
+    move("s", B("outb", 1536, 3072), IND(B("xb", 0, 3 * CW), B("su", 96, 192)))
+    move("v", B("outb", 0, 1536), IND(B("xb", 0, 3 * CW), B("su", 0, 96)))
+    first, end = (48 if up else 0), (3024 if down else 3072)
+    dma("s", None, B("outb", 1536, end), "o1", out_ap=T.yx[:, 1536:end])
+    dma("y", None, B("outb", first, 1536), "o2", out_ap=T.yx[:, first:1536])
+    ts(n2, ni, 8191, AND)
+    ts(n3, ni, 57344, AND)
+    ts(n1, n2, -4096.0, A.add, float(INV), A.mult)
+    ts(n2, n1, 4096.0, A.add)
+    ts(n1, n2, 8191, AND)
+    for c in range(3):
+        tt(B("yn", c, 192, 3), B("n1", 64 * c, 64 * c + 64), B("n3", 64 * c, 64 * c + 64), A.add)
+    for i, o in meeting(1):
+        tt(B("fin", 48 * i, 48 * i + 48), B("tx1", TS[i], TS[i] + 48), B("mm", 48 * i, 48 * i + 48), A.subtract if i else A.add)
+        tt(B("yn", 189 * i, 189 * i + 3), o, B("nm", 3 * i, 3 * i + 3), A.add)
+    if up:
+        dma("s", None, B("fin", 0, 48), "o3", out_ap=T.yx[:, 0:48])
+    if down:
+        dma("y", None, B("fin", 48, 96), "o4", out_ap=T.yx[:, 3024:3072])
+    dma("y" if up else "s", None, B("yn", 0, 192), "o5", out_ap=T.yb[:])
+    for sem in sorted(count):
+        if count[sem]:
+            need("g", sem, count[sem])

@@ -6,9 +6,10 @@ ACT = ActivationFunctionType
 AND, SHR = A.bitwise_and, A.logical_shift_right
 C = float(2 ** 25)
 HUGE = float(2 ** 60)
+ONE = 131072.0
 CW = 1040
-NV = 30
-NA = 18
+NV, NV0, NV1 = 30, 44, 40
+PARTS = ((0, 1), (2,))
 
 
 def centred(v):
@@ -23,23 +24,26 @@ F, H, I, U = "float32", "bfloat16", "int32", "uint16"
 SCRATCH = {}
 for _n, _w, _t in (("xn", 3072, H), ("outb", 3072, H), ("ew", 8192, H), ("bt", 192, I), ("xa", 3 * CW, H), ("xb", 3 * CW, H), ("sel", 2048, H),
                    ("jb0", 128, H), ("jb1", 128, H), ("jb", 128, H), ("one", 128, H), ("idp", 128, H), ("idn", 128, H), ("blk", 128, H),
-                   ("kc", 64, H), ("kcb", 64, H), ("pi", 1, I), ("pj", 1, I), ("sv", 8, F), ("io48", 64, I), ("iob", 64, I),
-                   ("pos", 64, F), ("zero", 64, F), ("neg", 64, H), ("rl", 192, U), ("n1", 192, I), ("n2", 192, I), ("n3", 192, I),
-                   ("wf", 192, I), ("ni", 192, I), ("so", 192, I), ("su", 192, U), ("h1", 6, I), ("h2", 6, I), ("h3", 6, I), ("hu", 6, U), ("hw", 6, I),
-                   ("q1", 6, I), ("q2", 6, I), ("bu", 12, U), ("mc", 96, F), ("mm", 96, F), ("mcmp", 96, H), ("mw", 96, F), ("fin", 96, H),
-                   ("nd", 6, F), ("nw", 6, F), ("nm", 6, F), ("pn", 12, F), ("p1", 12, I), ("p2", 12, I), ("p3", 12, I), ("yn", 192, F), ("db", 96, H),
-                   ("tx0", 108, F), ("tx1", 108, F), ("rx0", 108, F), ("rx1", 108, F), ("xo", 3 * 16 * NV, H)):
+                   ("pi", 1, I), ("pj", 1, I), ("sv", 8, F), ("io48", 64, I), ("iob", 64, I),
+                   ("pos", 192, F), ("zero", 192, F), ("rst", 192, F), ("neg", 192, H), ("rl", 192, U), ("n1", 192, I), ("n2", 192, I), ("n3", 192, I),
+                   ("wf", 192, I), ("ni", 192, I), ("so", 192, I), ("su", 192, U), ("h1", 6, I), ("h2", 6, I), ("h3", 6, I), ("hu", 12, U), ("hw", 6, I),
+                   ("q1", 12, I), ("q2", 12, I), ("mc", 192, F), ("mm", 96, F), ("mcmp", 192, H), ("mw", 192, F), ("fin", 96, H), ("xe", 96, H),
+                   ("wa", 3, F), ("uf", 3, F), ("nd", 12, F), ("nw", 12, F), ("nm", 12, F), ("zz", 12, F), ("dz", 6, F), ("zm", 6, F),
+                   ("pn", 6, F), ("p1", 6, I), ("p2", 6, I), ("p3", 6, I), ("yn", 192, F),
+                   ("tx0", 108, F), ("tx1", 108, F), ("rx0", 108, F), ("rx1", 108, F), ("xo", 3 * 16 * NV, H),
+                   ("s", 192, F), ("xk", 192, F), ("t", 192, F), ("nk", 192, F), ("ys", 192, F), ("ra", 192, F), ("rb", 192, F), ("ma", 192, H), ("mb", 192, H),
+                   ("sg", 192, H), ("cs", 192, I), ("ca", 192, I), ("oi", 192, I), ("cu", 192, U), ("of", 192, U)):
     SCRATCH[_n] = ("sbuf", [128, _w], _t)
 for _c in range(3):
-    for _n, _w, _t in (("s", 64, F), ("x", 64, F), ("t", 64, F), ("nm", 64, F), ("ys", 64, F), ("ra", 64, F), ("rb", 64, F), ("ma", 64, H), ("mb", 64, H),
-                       ("sg", 64, H), ("cs", 64, I), ("ca", 64, I), ("oi", 64, I), ("cu", 64, U), ("of", 64, U),
-                       ("dv", 1008, H), ("cmp", 1008, H), ("xr", 1008, H), ("es", 1008, H)):
-        SCRATCH["%s_%d" % (_n, _c)] = ("sbuf", [128, _w], _t)
-PSUM = ("va", "vb", "z0", "z1", "z2", "u0", "u1", "u2")
+    for _n in ("dv", "cmp", "xr", "es"):
+        SCRATCH["%s_%d" % (_n, _c)] = ("sbuf", [128, 1008], H)
+for _c in sorted(set((NV, NV0, NV1))):
+    SCRATCH["kc%d" % _c] = ("sbuf", [128, 64], H)
+PSUM = ("va", "vb", "z0", "z1", "u0", "u1", "u2", "u3")
 for _n in PSUM:
     SCRATCH[_n] = ("psum", [128, 512], F)
 QSEM = {"v": "qv", "s": "qs", "p": "qp", "g": "qg"}
-SEMAPHORES = ["qv", "qs", "qp", "qg", "db", "dx", "de", "o1", "o2", "o3", "o4", "o5", "rh0", "rf0", "rh1", "rf1", "loc"]
+SEMAPHORES = ["qv", "qs", "qp", "qg", "db", "dx", "de", "o1", "o2", "o3", "o4", "o5", "o6", "rh0", "rf0", "rh1", "rf1", "loc"]
 
 
 def B(name, a, b, step=1):
@@ -63,35 +67,33 @@ def win(x, c):
     return B(x, c * CW, (c + 1) * CW)
 
 
-def Y(c, a=0, b=64):
-    return B("va", 64 * c + a, 64 * c + b)
+def Y(a, b, step=1):
+    return B("va", a, b, step)
 
 
-def ACC(c):
-    return B("va", 192 + 64 * c, 256 + 64 * c)
+def ACC(a, b, step=1):
+    return B("va", 192 + a, 192 + b, step)
 
 
-NBX, NBR = B("va", 385, 449), B("va", 384, 448, -1)
+def UT(a, b, step=1):
+    return B("vb", a, b, step)
 
 
-def UT(c, a=0, b=64):
-    return B("vb", 64 * c + a, 64 * c + b)
+def R(k):
+    return "rb" if k % 2 else "ra"
 
 
-def VT(c, step=1):
-    return B("vb", 192 + 64 * c, 256 + 64 * c, step)
+def M(k):
+    return "mb" if k % 2 else "ma"
 
 
-def t_(n, c, a=0, b=64, step=1):
+def t_(n, c, a, b, step=1):
     return B("%s_%d" % (n, c), a, b, step)
 
 
-def R(c, k, a=0, b=64):
-    return t_("rb" if k % 2 else "ra", c, a, b)
-
-
-def M(c, k, step=1):
-    return t_("mb" if k % 2 else "ma", c, 0, 64, step)
+def drain(calls, n=99):
+    for _ in zip(range(n), calls):
+        pass
 
 
 EW = B("ew", 0, 8192)
@@ -170,7 +172,7 @@ def rank_program(g, core, T, topo):
     def fill(out, val):
         op("v", [], [out], lambda: g.vector.memset(ap(out), val))
 
-    def act(out, a, func, **kw):
+    def act(out, a, func=ACT.Copy, **kw):
         op("s", [a], [out], lambda: g.scalar.activation(ap(out), ap(a), func, **kw))
 
     def mm(out, lhs, rhs, start, stop):
@@ -198,30 +200,33 @@ def rank_program(g, core, T, topo):
     gsel(B("jb1", 0, 128), B("jb0", 0, 128), [[-16, 8], [0, 16]], A.is_ge, -1.0, 0, 1)
     gsel(B("jb", 0, 128), B("jb1", 0, 128), [[16, 8], [0, 16]], A.is_ge, -1.0, 15, -1)
     gsel(IDP, B("one", 0, 128), [[-1, 128]], A.is_equal, 0.0, 0, 1)
-    fill(B("zero", 0, 64), 0.0)
-    fill(B("neg", 0, 64), -1.0)
+    for n, v in (("zero", 0.0), ("ra", 0.0), ("rb", 0.0), ("rst", 1.0), ("neg", -1.0)):
+        fill(B(n, 0, 192), v)
+    fill(B("rst", 0, 192, 64), 0.0)
     for c in range(3):
         fill(B("xa", c * CW, c * CW + 16), 512.0)
         fill(B("xb", c * CW, c * CW + 16), 512.0)
-    for k in ("kc", "kcb"):
+    for n in sorted(set((NV, NV0, NV1))):
+        k = "kc%d" % n
         fill(B(k, 0, 64), -7.0 * C)
-        fill(B(k, 1, 1 + NV), -11.5 * C)
+        fill(B(k, 1, 1 + n), -11.5 * C)
         fill(B(k, 0, 1), -float(2 ** 30))
-    fill(B("kcb", 63, 64), -11.5 * C)
-    fill(B("va", 448, 449), 0.0)
+    fill(B("vb", 448, 449), 0.0)
+    fill(B("tx0", 105, 108), 0.0)
+    fill(B("tx1", 105, 108), 0.0)
     ts(B("pj", 0, 1), B("pi", 0, 1), 15, AND)
     for c in range(3):
         ts(B("sv", c, c + 1), B("pj", 0, 1), float(CW * c), A.add)
         ts(B("sv", 4 + c, 5 + c), B("pj", 0, 1), float(16 * c), A.add)
     for c in range(3):
         ts(B("rl", 64 * c, 64 * c + 64), B("io48", 0, 64), B("sv", 4 + c, 5 + c), A.add)
-    ts(B("pos", 0, 64), B("iob", 0, 64), 131072.0, A.mult)
+        ts(B("pos", 64 * c, 64 * c + 64), B("iob", 0, 64), ONE, A.mult)
 
     def move(q, dst, src):
         if q == "v":
             cp(dst, src)
         else:
-            act(dst, src, ACT.Copy)
+            act(dst, src)
 
     def relay(q, c, b0, b1):
         move(q, own("xa", c, b0 - 1, b1 - 1), IND(B("xn", 0, 3072), B("rl", 64 * c + b0, 64 * c + b1)))
@@ -232,116 +237,149 @@ def rank_program(g, core, T, topo):
     def xo(c):
         return B("xo", 16 * NV * c, 16 * NV * (c + 1))
 
-    def place_words(c, a=0, b=64):
-        tt(Y(c, a, b), B("wf", 64 * c + a, 64 * c + b), B("pos", a, b), A.add)
-        e = min(b, 63)
-        if e > a:
-            cp(R(c, 0, a + 1, e + 1), Y(c, a, e))
+    def place_words():
+        tt(Y(0, 192), B("wf", 0, 192), B("pos", 0, 192), A.add)
+        cp(B("ra", 1, 192), Y(0, 191))
 
-    def first_list(c):
-        tt(t_("cs", c, 0, 63), UT(c, 1, 64), B("wf", 64 * c, 64 * c + 63), A.add)
-        ts(t_("ca", c, 0, 63), t_("cs", c, 0, 63), 8191, AND)
-        cp(t_("cu", c, 0, 63), t_("ca", c, 0, 63))
+    def first_list():
+        tt(B("cs", 0, 191), UT(1, 192), B("wf", 0, 191), A.add)
+        ts(B("ca", 0, 191), B("cs", 0, 191), 8191, AND)
+        cp(B("cu", 0, 191), B("ca", 0, 191))
 
     turn = [0]
 
     def bank():
         turn[0] += 1
-        return "u%d" % (turn[0] % 3)
+        return "u%d" % (turn[0] % 4)
 
-    def first_diff(x, c):
-        o = B(bank(), 0, 16 * NV)
-        mm(o, IDP, own(x, c, 0, NV, -1), True, False)
-        mm(o, IDN, own(x, c, 0, NV), False, True)
-        act(t_("dv", c, 0, 16 * NV), o, ACT.Copy)
+    def first_diff(x, c, nv):
+        for j0 in range(0, nv, 32):
+            j1 = min(j0 + 32, nv)
+            o = B(bank(), 0, 16 * (j1 - j0))
+            mm(o, IDP, own(x, c, j0, j1, -1), True, False)
+            mm(o, IDN, own(x, c, j0, j1), False, True)
+            act(t_("dv", c, 16 * j0, 16 * j1), o)
 
     def race_v_diff(x, c):
-        tt(t_("dv", c, 0, 16 * NV), IND(win(x, c), t_("of", c, 0, NV)), xo(c), A.subtract)
+        tt(t_("dv", c, 0, 16 * NV), IND(win(x, c), B("of", 64 * c, 64 * c + NV)), xo(c), A.subtract)
 
-    def race_v(c):
-        tt(t_("cmp", c, 0, 16 * NV), IND(EW, t_("cu", c, 0, NV)), t_("dv", c, 0, 16 * NV), A.is_gt)
+    def race_v(c, nv=NV):
+        tt(t_("cmp", c, 0, 16 * nv), IND(EW, B("cu", 64 * c, 64 * c + nv)), t_("dv", c, 0, 16 * nv), A.is_gt)
 
-    def race_s(x, c, k):
-        halves = ((bank(), NV, NV + NA), (bank(), NV + NA, 63))
+    def race_s(x, p, k, nv=NV):
+        na = nv + 2 * ((66 - nv) // 4)
+        signs = []
+
+        def enc(c, u, j0, j1):
+            act(t_("es", c, 16 * j0, 16 * j1), IND(EW, B("cu", 64 * c + j0, 64 * c + j1)))
+            mm(B(u, 0, 16 * (j1 - j0)), IDP, t_("es", c, 16 * j0, 16 * j1), False, True)
+
+        def sign():
+            for out, a in signs:
+                act(out, a, ACT.Sign, bias=-0.5)
+        for c in p:
+            halves = ((bank(), nv, na), (bank(), na, 63))
+            if k:
+                act(t_("xr", c, 16 * nv, 1008), IND(win(x, c), B("of", 64 * c + nv, 64 * c + 63)))
+            for i, (u, j0, j1) in enumerate(halves):
+                o = B(u, 0, 16 * (j1 - j0))
+                mm(o, IDP, own(x, c, j0, j1), True, False)
+                mm(o, IDN, t_("xr", c, 16 * j0, 16 * j1) if k else own(x, c, j0, j1, -1), False, False)
+                if not k:
+                    enc(c, u, j0, j1)
+                if i == (1 if k else 0):
+                    sign()
+            if k:
+                for u, j0, j1 in halves:
+                    enc(c, u, j0, j1)
+            signs[:] = [(t_("cmp", c, 16 * j0, 16 * j1), B(u, 0, 16 * (j1 - j0))) for u, j0, j1 in halves]
+        sign()
+
+    def zat(c, k, day):
+        return ("z1", 64 * c) if day and not k else ("z%d" % (c // 2), 64 * (c % 2))
+
+    def counts(c, k, day, nv=NV):
+        z, a = zat(c, k, day)
+        mm(B(z, a, a + 64), IDP, B("kc%d" % nv, 0, 64), True, False)
         if k:
-            act(t_("xr", c, 16 * NV, 1008), IND(win(x, c), t_("of", c, NV, 63)), ACT.Copy)
-        for p, j0, j1 in halves:
-            o = B(p, 0, 16 * (j1 - j0))
-            mm(o, IDP, own(x, c, j0, j1), True, False)
-            mm(o, IDN, t_("xr", c, 16 * j0, 16 * j1) if k else own(x, c, j0, j1, -1), False, False)
-            act(t_("es", c, 16 * j0, 16 * j1), IND(EW, t_("cu", c, j0, j1)), ACT.Copy)
-            mm(o, IDP, t_("es", c, 16 * j0, 16 * j1), False, True)
-        for p, j0, j1 in halves:
-            act(t_("cmp", c, 16 * j0, 16 * j1), B(p, 0, 16 * (j1 - j0)), ACT.Sign, bias=-0.5)
-
-    def counts(c, k, kc="kc"):
-        z = "z%d" % c
-        mm(B(z, 0, 64), IDP, B(kc, 0, 64), True, False)
-        if k:
-            mm(B(z, 0, 64), IDP, M(c, k), False, False)
+            mm(B(z, a + 1, a + 64), IDP, B(M(k), 64 * c + 1, 64 * c + 64), False, False)
         for s in range(16):
-            mm(B(z, 1, 64), B("sel", 128 * s, 128 * s + 128), t_("cmp", c, s, 1008, 16), False, s == 15)
+            mm(B(z, a + 1, a + 64), B("sel", 128 * s, 128 * s + 128), t_("cmp", c, s, 1008, 16), False, s == 15)
 
-    def post(c, k):
+    def post(p, k, day):
         last = k == 2
-        scan(t_("s", c), t_("sg", c) if k else B("neg", 0, 64), B("z%d" % c, 0, 64), -1.0, A.mult, A.min)
-        tt(VT(c), Y(c), t_("s", c), A.min)
-        scan(NBR, M(c, k, -1) if k else B("zero", 0, 64, -1), VT(c, -1), 0.0, A.min, A.max)
-        tt(t_("t", c), VT(c), R(c, k), A.min)
-        tt(t_("x", c), t_("s", c), NBX, A.max)
+        a, b = 64 * p[0], 64 * p[-1] + 64
+        n = b - a
+        zn, z = zat(p[0], k, day)
+        vt, vtr = B("vb", 192, 192 + n), B("vb", 192, 192 + n, -1)
+        nbx, nbr = B("vb", 449 - n, 449), B("vb", 448 - n, 448, -1)
+        s, t, x, nk, ys = (B(i, a, b) for i in ("s", "t", "xk", "nk", "ys"))
+        yield scan(s, B("sg" if k else "neg", a, b), B(zn, z, z + n), -1.0, A.mult, A.min)
+        yield tt(vt, Y(a, b), s, A.min)
+        yield scan(nbr, B(M(k) if k else "zero", a, b, -1), vtr, 0.0, A.min, A.max)
+        yield tt(t, vt, B(R(k), a, b), A.min)
+        yield tt(x, s, nbx, A.max)
         if k:
-            tt(t_("nm", c), NBX, M(c, k), A.subtract)
+            yield tt(nk, nbx, B(M(k), a, b), A.subtract)
         else:
-            tt(ACC(c), NBX, t_("t", c), A.max)
-        tt(t_("ys", c) if last else Y(c), Y(c), t_("x", c), A.subtract)
+            yield tt(ACC(a, b), nbx, t, A.max)
+        yield tt(ys if last else Y(a, b), Y(a, b), x, A.subtract)
         if k:
-            tt(ACC(c), ACC(c), t_("t", c), A.max)
+            yield tt(ACC(a, b), ACC(a, b), t, A.max)
         if not last:
-            scan(R(c, k + 1, 1, 64), Y(c, 0, 63), B("zero", 0, 63), 0.0, A.max, A.max)
+            yield scan(B(R(k + 1), a + 1, b), B("rst", a, b - 1), Y(a, b - 1), 0.0, A.mult, A.max)
         if k:
-            tt(ACC(c), ACC(c), t_("nm", c), A.max)
+            yield tt(ACC(a, b), ACC(a, b), nk, A.max)
         if last:
-            tt(ACC(c), ACC(c), t_("ys", c), A.max)
+            yield tt(ACC(a, b), ACC(a, b), ys, A.max)
             return
-        tt(t_("cs", c, 0, 63), UT(c, 1, 64), R(c, k + 1, 1, 64), A.add)
-        ts(M(c, k + 1), Y(c), 0.0, A.is_le, HUGE, A.mult)
-        ts(t_("oi", c, 0, 63), t_("cs", c, 0, 63), 13, SHR, 0x7F0, AND)
-        ts(t_("ca", c, 0, 63), t_("cs", c, 0, 63), 8191, AND)
-        ts(t_("of", c, 0, 63), t_("oi", c, 0, 63), B("sv", 0, 1), A.add)
-        cp(t_("cu", c, 0, 63), t_("ca", c, 0, 63))
+        cs, oi, ca = B("cs", a, b - 1), B("oi", a, b - 1), B("ca", a, b - 1)
+        yield tt(cs, UT(a + 1, b), B(R(k + 1), a + 1, b), A.add)
+        yield ts(B(M(k + 1), a, b), Y(a, b), 0.0, A.is_le, HUGE, A.mult)
+        yield ts(oi, cs, 13, SHR, 0x7F0, AND)
+        yield ts(ca, cs, 8191, AND)
+        yield ts(B("of", a, b - 1), oi, B("sv", 0, 1), A.add)
+        yield cp(B("cu", a, b - 1), ca)
 
-    def later_intervals(x):
+    def later_intervals(x, day):
         for k in range(2):
-            for c in range(3):
-                post(c, k)
-                race_v_diff(x, c)
-                ts(t_("sg", c), M(c, k + 1), 2.0 / HUGE, A.mult, -1.0, A.add)
+            todo = [post(p, k, day) for p in PARTS]
+            for i, p in enumerate(PARTS):
+                a, b = 64 * p[0], 64 * p[-1] + 64
+                drain(todo[i])
+                rest = todo[i + 1] if i + 1 < len(PARTS) else iter(())
+                for c in p:
+                    race_v_diff(x, c)
+                    drain(rest, 1)
+                ts(B("sg", a, b), B(M(k + 1), a, b), 2.0 / HUGE, A.mult, -1.0, A.add)
+                for c in p:
+                    race_v(c)
+                    drain(rest, 1)
+                race_s(x, p, k + 1)
+                for c in p:
+                    counts(c, k + 1, day)
                 if k == 0:
-                    ts(UT(c), UT(c), 811.0, A.add)
-                race_v(c)
-                race_s(x, c, k + 1)
-                counts(c, k + 1)
+                    ts(UT(a, b), UT(a, b), 811.0, A.add)
 
-    TS, TW, TU = (6, 54), (0, 102), (3, 105)
-    RS, RW, RU = (0, 60), (48, 54), (51, 57)
+    TS, TW, TU = (6, 54), (0, 102), 3
+    RS, RW, RU = (0, 60), (48, 54), 57
 
     def heads_and_feet(day, x):
         tx = "tx%d" % day
-        h1, h2, h3, hw = B("h1", 0, 6), B("h2", 0, 6), B("h3", 0, 6), B("hw", 0, 6)
-        cp(B("h1", 0, 3), B("va", 192, 384, 64))
-        cp(B("h1", 3, 6), B("va", 192 + 63, 384, 64))
+        h1, h2 = B("h1", 0, 6), B("h2", 0, 6)
+        cp(B("h1", 0, 3), ACC(0, 192, 64))
+        cp(B("h1", 3, 6), ACC(63, 192, 64))
         ts(h2, h1, 13, SHR, 0x7F0, AND)
-        ts(hw, h1, 65535, AND)
+        ts(B("h3", 0, 3), B("h1", 0, 3), 8191, AND)
         for c in range(3):
             ts(B("hu", c, 6, 3), B("h2", c, 6, 3), B("sv", c, c + 1), A.add)
-        ts(h3, h1, 8191, AND)
+        ts(B("hw", 0, 6), h1, 65535, AND)
         cp(B(tx, 6, 102), IND(B(x, 0, 3 * CW), B("hu", 0, 6)))
-        ts(h1, h3, -4096.0, A.add, float(BETA), A.mult)
+        ts(B("h1", 0, 3), B("h3", 0, 3), -4096.0, A.add, float(BETA), A.mult)
         for i in range(2):
             cp(B(tx, TW[i], TW[i] + 3), B("hw", 3 * i, 3 * i + 3))
-        ts(h3, h1, 8191, AND)
-        for i in range(2):
-            cp(B(tx, TU[i], TU[i] + 3), B("h3", 3 * i, 3 * i + 3))
+        ts(B("h3", 0, 3), B("h1", 0, 3), 8191, AND)
+        ts(B(tx, TU, TU + 3), B("h3", 0, 3), float(4096 + 811 * (6 + day)), A.add)
 
     def send(day):
         tx, rx = "tx%d" % day, "rx%d" % day
@@ -362,69 +400,110 @@ def rank_program(g, core, T, topo):
                 count[sem] = len(topo.engines(T.cores[r], core)) // fan
                 log.setdefault(rx, []).append(("w", a, a + 54, "remote", sem, count[sem]))
 
-    parts = [i for i, ok in ((0, up), (1, down)) if ok]
-    lo, hi = 48 * parts[0], 48 * parts[-1] + 48
-    la, lb = lo // 16, hi // 16
-
-    def decode(n0, n1):
-        p1, p2, p3 = B("p1", n0, n1), B("p2", n0, n1), B("p3", n0, n1)
-        ts(p2, p1, 8191, AND)
-        ts(p3, p1, 57344, AND)
-        ts(p1, p2, -4096.0, A.add, float(INV), A.mult)
-        ts(p2, p1, 4096.0, A.add)
-        ts(p1, p2, 8191, AND)
-        tt(B("pn", n0, n1), p1, p3, A.add)
+    sides = [i for i, ok in ((0, up), (1, down)) if ok]
 
     def meeting(day):
         tx, rx = "tx%d" % day, "rx%d" % day
-        for i in parts:
-            hd, ft = (tx, rx) if i == 0 else (rx, tx)
-            u, w = (TU if i == 0 else RU)[i], (RW if i == 0 else TW)[i]
-            tt(B("nm", 3 * i, 3 * i + 3), B(hd, u, u + 3), B(ft, w, w + 3), A.add)
-        ts(B("q1", la, lb), B("nm", la, lb), float(4096 + 811 * (6 + day)), A.add)
-        for i in parts:
-            o, r = B(tx, TS[i], TS[i] + 48), B(rx, RS[i], RS[i] + 48)
-            tt(B("mc", 48 * i, 48 * i + 48), o if i else r, r if i else o, A.subtract)
+        nb = 1 if day else 2
+        la, lb = 3 * nb * sides[0], 3 * nb * sides[-1] + 3 * nb
+        lo, hi = 16 * la, 16 * lb
+        for i in sides:
+            l = 3 * nb * i
+            u = B(rx, RU, RU + 3) if i else B(tx, TU, TU + 3)
+            w = B(tx, TW[1], TW[1] + 3) if i else B(rx, RW[0], RW[0] + 3)
+            tt(B("q1", l, l + 3), u, w, A.add)
+            if not day:
+                tt(B("q1", l + 3, l + 6), u if i else UT(1, 192, 64), B("wa", 0, 3) if i else w, A.add)
         ts(B("q2", la, lb), B("q1", la, lb), 8191, AND)
-        cp(B("hu", 0, lb - la), B("q2", la, lb))
+        for i in sides:
+            l = 48 * nb * i
+            o, r = B(tx, TS[i], TS[i] + 48), B(rx, RS[i], RS[i] + 48)
+            tt(B("mc", l, l + 48), o if i else r, r if i else o, A.subtract)
+            if i == sides[0]:
+                cp(B("hu", 0, lb - la), B("q2", la, lb))
+            if not day:
+                e = B("xe", 48 * i, 48 * i + 48)
+                tt(B("mc", l + 48, l + 96), e if i else r, r if i else e, A.subtract)
         tt(B("mcmp", lo, hi), IND(EW, B("hu", 0, lb - la)), B("mc", lo, hi), A.is_gt)
-        mm(B("z0", lo, hi), B("blk", 0, 128), B("mcmp", lo, hi), True, True)
+        u0, u1 = bank(), bank()
+        mm(B(u0, lo, hi), B("blk", 0, 128), B("mcmp", lo, hi), True, True)
         for s in range(16):
-            mm(B("z1", la, lb), B("sel", 128 * s, 128 * s + 128), B("mcmp", lo + s, hi, 16), s == 0, s == 15)
+            mm(B(u1, la, lb), B("sel", 128 * s, 128 * s + 128), B("mcmp", lo + s, hi, 16), s == 0, s == 15)
+        return u0, u1
+
+    def outcome(day, u0, u1):
+        tx, rx = "tx%d" % day, "rx%d" % day
+        nb = 1 if day else 2
+        la, lb = 3 * nb * sides[0], 3 * nb * sides[-1] + 3 * nb
+        lo, hi = 16 * la, 16 * lb
+        if not day:
+            for i in sides:
+                tt(B("nd", 6 * i, 6 * i + 3), B(rx, RW[i], RW[i] + 3), B(tx, TW[i], TW[i] + 3), A.subtract)
+            if down:
+                tt(B("nd", 9, 12), B(rx, RU, RU + 3), B("uf", 0, 3), A.subtract)
+        ts(B("mw", lo, hi), B(u0, lo, hi), 11.5, A.is_gt)
+        for i in sides:
+            l = 48 * nb * i
+            tt(B("mm", 48 * i, 48 * i + 48), B("mw", l, l + 48), B("mc", l, l + 48), A.mult)
+        for i in sides:
+            sub = A.subtract if i else A.add
+            if day:
+                tt(B("fin", 48 * i, 48 * i + 48), B(tx, TS[i], TS[i] + 48), B("mm", 48 * i, 48 * i + 48), sub)
+                continue
+            for c in range(3):
+                a, b = TS[i] + 16 * c, 48 * i + 16 * c
+                tt(own("xb", c, 63 * i - 1, 63 * i), B(tx, a, a + 16), B("mm", b, b + 16), sub)
         if day:
-            for i in parts:
-                cp(B("p1", 6 * i, 6 * i + 3), B(tx, TW[i], TW[i] + 3))
-                cp(B("p1", 6 * i + 3, 6 * i + 6), B(rx, RW[i], RW[i] + 3))
-            decode(6 * parts[0], 6 * parts[-1] + 6)
-        src = []
-        for i in parts:
-            o = B("pn", 6 * i, 6 * i + 3) if day else B(tx, TW[i], TW[i] + 3)
-            r = B("pn", 6 * i + 3, 6 * i + 6) if day else B(rx, RW[i], RW[i] + 3)
-            tt(B("nd", 3 * i, 3 * i + 3), r, o, A.subtract)
-            src.append((i, o))
-        ts(B("mw", lo, hi), B("z0", lo, hi), 11.5, A.is_gt)
-        ts(B("nw", la, lb), B("z1", la, lb), 11.5 * C, A.is_gt)
-        tt(B("mm", lo, hi), B("mw", lo, hi), B("mc", lo, hi), A.mult)
-        tt(B("nm", la, lb), B("nw", la, lb), B("nd", la, lb), A.mult)
-        return src
+            for i in sides:
+                cp(B("p1", 3 * i, 3 * i + 3), B(rx, RW[i], RW[i] + 3))
+            a, b = 3 * sides[0], 3 * sides[-1] + 3
+            p1, p2, p3 = B("p1", a, b), B("p2", a, b), B("p3", a, b)
+            ts(p2, p1, 8191, AND)
+            ts(p3, p1, 57344, AND)
+            ts(p1, p2, -4096.0, A.add, float(INV), A.mult)
+            ts(B("nw", a, b), B(u1, a, b), 11.5 * C, A.is_gt)
+            ts(p2, p1, 8191, AND)
+            tt(B("pn", a, b), p2, p3, A.add)
+            for i in sides:
+                tt(B("nd", 3 * i, 3 * i + 3), B("pn", 3 * i, 3 * i + 3), B("yn", 189 * i, 189 * i + 3), A.subtract)
+            tt(B("nm", a, b), B("nw", a, b), B("nd", a, b), A.mult)
+            for i in sides:
+                y = B("yn", 189 * i, 189 * i + 3)
+                tt(y, y, B("nm", 3 * i, 3 * i + 3), A.add)
+            return
+        ts(B("nw", la, lb), B(u1, la, lb), 11.5 * C, A.is_gt)
+        ts(B("zz", la, lb), B(u1, la, lb), -11.5 * C, A.add)
+        for i in sides:
+            z = B("z1", 62 * i + 1, 192, 64)
+            tt(B("dz", 3 * i, 3 * i + 3), B("zz", 6 * i + 3, 6 * i + 6), z, A.subtract)
+        for i in sides:
+            tt(B("nm", 6 * i, 6 * i + 3), B("nw", 6 * i, 6 * i + 3), B("nd", 6 * i, 6 * i + 3), A.mult)
+            tt(B("zm", 3 * i, 3 * i + 3), B("nw", 6 * i, 6 * i + 3), B("dz", 3 * i, 3 * i + 3), A.mult)
+        for i in sides:
+            z, y = B("z1", 62 * i + 1, 192, 64), Y(63 * i, 192, 64)
+            tt(y, y, B("nm", 6 * i, 6 * i + 3), A.add)
+            tt(z, z, B("zm", 3 * i, 3 * i + 3), A.add)
+        if down:
+            tt(B("nm", 9, 12), B("nw", 6, 9), B("nd", 9, 12), A.mult)
+        if up:
+            cp(B("ra", 1, 192, 64), Y(0, 192, 64))
+        if down:
+            tt(UT(63, 192, 64), UT(63, 192, 64), B("nm", 9, 12), A.add)
 
     n1, n2, n3 = B("n1", 0, 192), B("n2", 0, 192), B("n3", 0, 192)
-    ni, wf, ut = B("ni", 0, 192), B("wf", 0, 192), B("vb", 0, 192)
+    ni, wf, ut = B("ni", 0, 192), B("wf", 0, 192), UT(0, 192)
     for c in range(3):
         cp(B("n1", 64 * c, 64 * c + 64), B("bt", c, 192, 3))
-    ts(n2, n1, 101.0, A.mult)
+    ts(n2, n1, 101.0, A.mult, 4096.0, A.add)
     ts(n3, n1, 57344, AND)
     ts(ni, n2, 8191, AND)
-    ts(n2, n1, 37.0, A.mult)
+    ts(n2, n1, 37.0, A.mult, 4096.0, A.add)
     tt(wf, ni, n3, A.add)
     ts(n3, n2, 8191, AND)
     cp(ut, n3)
-    for c in range(3):
-        place_words(c)
-        fill(R(c, 0, 0, 1), 0.0)
-        fill(R(c, 1, 0, 1), 0.0)
-        first_list(c)
-        ts(UT(c), UT(c), 811.0, A.add)
+    first_list()
+    place_words()
+    ts(ut, ut, 811.0, A.add)
     relay("s", 0, 0, 64)
     relay("v", 1, 0, 64)
     relay("s", 2, 0, 32)
@@ -434,30 +513,32 @@ def rank_program(g, core, T, topo):
     for s in range(16):
         ts(B("sel", 128 * s, 128 * s + 128), B("jb", 0, 128), float(s), A.is_equal, C, A.mult)
     for c in range(3):
-        first_diff("xa", c)
+        first_diff("xa", c, NV0)
         cp(xo(c), own("xa", c, 0, NV))
     for c in range(3):
-        race_v(c)
-        race_s("xa", c, 0)
-        counts(c, 0)
-    later_intervals("xa")
+        race_v(c, NV0)
+    race_s("xa", (0, 1), 0, NV0)
+    counts(0, 0, 0, NV0)
+    race_s("xa", (2,), 0, NV0)
+    counts(1, 0, 0, NV0)
+    counts(2, 0, 0, NV0)
+    later_intervals("xa", 0)
 
-    def source(c):
-        sl = (64 * c, 64 * c + 64)
-        cp(B("ni", *sl), ACC(c))
-        ts(B("so", *sl), B("ni", *sl), 13, SHR, 0x7F0, AND)
+    def source(a, b):
+        cp(B("ni", a, b), ACC(a, b))
+        ts(B("so", a, b), B("ni", a, b), 13, SHR, 0x7F0, AND)
 
-    def source_list(c):
-        source(c)
-        ts(B("su", 64 * c, 64 * c + 64), B("so", 64 * c, 64 * c + 64), B("sv", 0, 1), A.add)
-    for c in range(3):
-        post(c, 2)
-        if c < 2:
-            source_list(c)
-            perm("s", c, 0, 64)
+    def source_list(a, b):
+        source(a, b)
+        ts(B("su", a, b), B("so", a, b), B("sv", 0, 1), A.add)
+    drain(post(PARTS[0], 2, 0))
+    source_list(0, 128)
+    perm("s", 0, 0, 64)
+    perm("s", 1, 0, 64)
+    drain(post(PARTS[1], 2, 0))
     heads_and_feet(0, "xa")
     send(0)
-    source_list(2)
+    source_list(128, 192)
     perm("s", 2, 32, 64)
     perm("v", 2, 0, 32)
 
@@ -466,67 +547,49 @@ def rank_program(g, core, T, topo):
     ts(n3, n2, -4096.0, A.add, float(BETA), A.mult)
     ts(n2, n3, 8191, AND)
     ts(ut, n2, float(4096 + 811 * 3), A.add)
+    first_list()
     for c in range(3):
-        first_diff("xb", c)
+        first_diff("xb", c, NV1)
     for c in range(3):
-        first_list(c)
-        race_s("xb", c, 0)
+        race_v(c, NV1)
+    race_s("xb", (0, 1), 0, NV1)
+    counts(0, 0, 1, NV1)
     for c in range(3):
-        race_v(c)
+        act(B("xe", 16 * c, 16 * c + 16), own("xb", c, 0, 1))
+        act(B("xe", 48 + 16 * c, 64 + 16 * c), own("xb", c, 61, 62))
+    race_s("xb", (2,), 0, NV1)
+    counts(1, 0, 1, NV1)
+    place_words()
+    ts(B("wa", 0, 3), B("wf", 62, 192, 64), float((811 * (3 - 6)) % 8192), A.add)
+    ts(B("uf", 0, 3), UT(63, 192, 64), float(811 * (6 - 3)), A.add)
+    banks = meeting(0)
+    counts(2, 0, 1, NV1)
     for c in range(3):
-        place_words(c)
-        cp(xo(c), own("xb", c, 0, NV))
-    for i, o in meeting(0):
-        for c in range(3):
-            tt(own("xb", c, 63 * i - 1, 63 * i), B("tx0", TS[i] + 16 * c, TS[i] + 16 * c + 16), B("mm", 48 * i + 16 * c, 48 * i + 16 * c + 16), A.subtract if i else A.add)
-        tt(B("wf", 63 * i, 192, 64), o, B("nm", 3 * i, 3 * i + 3), A.add)
-    if down:
-        ts(B("h2", 0, 3), B("wf", 63, 192, 64), 8191, AND)
-        ts(B("h1", 0, 3), B("h2", 0, 3), -4096.0, A.add, float(BETA), A.mult)
-        ts(B("h2", 0, 3), B("h1", 0, 3), 8191, AND)
-        ts(B("vb", 63, 192, 64), B("h2", 0, 3), float(4096 + 811 * 3), A.add)
-    tt(B("q1", 0, 3), B("vb", 1, 192, 64), B("wf", 0, 192, 64), A.add)
-    tt(B("q1", 3, 6), B("vb", 63, 192, 64), B("wf", 62, 192, 64), A.add)
-    ts(B("q2", 0, 6), B("q1", 0, 6), 8191, AND)
-    cp(B("bu", 0, 12, 2), B("q2", 0, 6))
-    ends = [(c, j, 16 * (c + i), 2 * (c + i)) for c in range(3) for i, j in ((0, 0), (3, 62))]
-    for c, j, a, l in ends:
-        tt(B("db", a, a + 16), own("xb", c, j, j + 1, -1), own("xb", c, j, j + 1), A.subtract)
-    for c, j, a, l in ends:
-        tt(t_("cmp", c, 16 * j, 16 * j + 16), IND(EW, B("bu", l, l + 1)), B("db", a, a + 16), A.is_gt)
-        if j:
-            counts(c, 0, "kcb")
-    for c in range(3):
-        place_words(c, 0, 1)
-        place_words(c, 63, 64)
-        ts(UT(c), UT(c), 811.0, A.add)
-    later_intervals("xb")
+        act(xo(c), own("xb", c, 0, NV))
+    outcome(0, *banks)
+    ts(ut, ut, 811.0, A.add)
+    later_intervals("xb", 1)
 
-    def final_source(c):
-        source(c)
-        ts(B("su", c, 192, 3), B("so", 64 * c, 64 * c + 64), B("sv", c, c + 1), A.add)
-    for c in range(3):
-        post(c, 2)
-        if c < 2:
-            final_source(c)
+    drain(post(PARTS[0], 2, 1))
+    drain(post(PARTS[1], 2, 1))
     heads_and_feet(1, "xb")
     send(1)
-    final_source(2)
-    move("s", B("outb", 1536, 3072), IND(B("xb", 0, 3 * CW), B("su", 96, 192)))
-    move("v", B("outb", 0, 1536), IND(B("xb", 0, 3 * CW), B("su", 0, 96)))
+    source(0, 192)
+    for c in range(3):
+        ts(B("su", c, 192, 3), B("so", 64 * c, 64 * c + 64), B("sv", c, c + 1), A.add)
     first, end = (48 if up else 0), (3024 if down else 3072)
-    dma("s", None, B("outb", 1536, end), "o1", out_ap=T.yx[:, 1536:end])
-    dma("y", None, B("outb", first, 1536), "o2", out_ap=T.yx[:, first:1536])
+    for q, a in (("s", 1024), ("s", 2048), ("v", 0)):
+        move(q, B("outb", a, a + 1024), IND(B("xb", 0, 3 * CW), B("su", a // 16, a // 16 + 64)))
+    dma("y", None, B("outb", 1024, 2048), "o1", out_ap=T.yx[:, 1024:2048])
+    dma("y", None, B("outb", first, 1024), "o2", out_ap=T.yx[:, first:1024])
+    dma("s", None, B("outb", 2048, end), "o6", out_ap=T.yx[:, 2048:end])
     ts(n2, ni, 8191, AND)
     ts(n3, ni, 57344, AND)
     ts(n1, n2, -4096.0, A.add, float(INV), A.mult)
-    ts(n2, n1, 4096.0, A.add)
-    ts(n1, n2, 8191, AND)
+    ts(n2, n1, 8191, AND)
     for c in range(3):
-        tt(B("yn", c, 192, 3), B("n1", 64 * c, 64 * c + 64), B("n3", 64 * c, 64 * c + 64), A.add)
-    for i, o in meeting(1):
-        tt(B("fin", 48 * i, 48 * i + 48), B("tx1", TS[i], TS[i] + 48), B("mm", 48 * i, 48 * i + 48), A.subtract if i else A.add)
-        tt(B("yn", 189 * i, 189 * i + 3), o, B("nm", 3 * i, 3 * i + 3), A.add)
+        tt(B("yn", c, 192, 3), B("n2", 64 * c, 64 * c + 64), B("n3", 64 * c, 64 * c + 64), A.add)
+    outcome(1, *meeting(1))
     if up:
         dma("s", None, B("fin", 0, 48), "o3", out_ap=T.yx[:, 0:48])
     if down:

@@ -8,7 +8,7 @@ C = float(2 ** 25)
 HUGE = float(2 ** 60)
 ONE = 131072.0
 CW = 1040
-NV, NV0, NV1 = 30, 44, 40
+NV, NV0, NV1 = 28, 44, 44
 PARTS = ((0, 1), (2,))
 
 
@@ -26,10 +26,11 @@ for _n, _w, _t in (("xn", 3072, H), ("outb", 3072, H), ("ew", 8192, H), ("bt", 1
                    ("jb0", 128, H), ("jb1", 128, H), ("jb", 128, H), ("one", 128, H), ("idp", 128, H), ("idn", 128, H), ("blk", 128, H),
                    ("pi", 1, I), ("pj", 1, I), ("sv", 8, F), ("io48", 64, I), ("iob", 64, I),
                    ("pos", 192, F), ("zero", 192, F), ("rst", 192, F), ("neg", 192, H), ("rl", 192, U), ("n1", 192, I), ("n2", 192, I), ("n3", 192, I),
-                   ("wf", 192, I), ("ni", 192, I), ("so", 192, I), ("su", 192, U), ("h1", 6, I), ("h2", 6, I), ("h3", 6, I), ("hu", 12, U), ("hw", 6, I),
+                   ("wf", 192, I), ("ni", 192, I), ("so", 192, I), ("su", 192, U), ("h1", 6, I), ("h2", 6, I), ("h3", 3, I), ("h4", 3, I), ("h5", 3, I),
+                   ("hu", 12, U), ("hw", 6, I),
                    ("q1", 12, I), ("q2", 12, I), ("mc", 192, F), ("mm", 96, F), ("mcmp", 192, H), ("mw", 192, F), ("fin", 96, H), ("xe", 96, H),
                    ("wa", 3, F), ("uf", 3, F), ("nd", 12, F), ("nw", 12, F), ("nm", 12, F), ("zz", 12, F), ("dz", 6, F), ("zm", 6, F),
-                   ("pn", 6, F), ("p1", 6, I), ("p2", 6, I), ("p3", 6, I), ("yn", 192, F),
+                   ("pn", 6, F), ("p1", 6, I), ("p2", 6, I), ("p3", 6, I), ("p4", 6, I), ("yn", 192, F),
                    ("tx0", 108, F), ("tx1", 108, F), ("rx0", 108, F), ("rx1", 108, F), ("xo", 3 * 16 * NV, H),
                    ("s", 192, F), ("xk", 192, F), ("t", 192, F), ("nk", 192, F), ("ys", 192, F), ("ra", 192, F), ("rb", 192, F), ("ma", 192, H), ("mb", 192, H),
                    ("sg", 192, H), ("cs", 192, I), ("ca", 192, I), ("oi", 192, I), ("cu", 192, U), ("of", 192, U)):
@@ -65,6 +66,10 @@ def own(x, c, j0, j1, shift=0):
 
 def win(x, c):
     return B(x, c * CW, (c + 1) * CW)
+
+
+def xo(c, j0=0, j1=NV):
+    return B("xo", 16 * (NV * c + j0), 16 * (NV * c + j1))
 
 
 def Y(a, b, step=1):
@@ -234,17 +239,14 @@ def rank_program(g, core, T, topo):
     def perm(q, c, b0, b1):
         move(q, own("xb", c, b0 - 1, b1 - 1), IND(win("xa", c), B("su", 64 * c + b0, 64 * c + b1)))
 
-    def xo(c):
-        return B("xo", 16 * NV * c, 16 * NV * (c + 1))
-
     def place_words():
-        tt(Y(0, 192), B("wf", 0, 192), B("pos", 0, 192), A.add)
-        cp(B("ra", 1, 192), Y(0, 191))
+        yield tt(Y(0, 192), B("wf", 0, 192), B("pos", 0, 192), A.add)
+        yield cp(B("ra", 1, 192), Y(0, 191))
 
     def first_list():
-        tt(B("cs", 0, 191), UT(1, 192), B("wf", 0, 191), A.add)
-        ts(B("ca", 0, 191), B("cs", 0, 191), 8191, AND)
-        cp(B("cu", 0, 191), B("ca", 0, 191))
+        yield tt(B("cs", 0, 191), UT(1, 192), B("wf", 0, 191), A.add)
+        yield ts(B("ca", 0, 191), B("cs", 0, 191), 8191, AND)
+        yield cp(B("cu", 0, 191), B("ca", 0, 191))
 
     turn = [0]
 
@@ -260,11 +262,15 @@ def rank_program(g, core, T, topo):
             mm(o, IDN, own(x, c, j0, j1), False, True)
             act(t_("dv", c, 16 * j0, 16 * j1), o)
 
-    def race_v_diff(x, c):
-        tt(t_("dv", c, 0, 16 * NV), IND(win(x, c), B("of", 64 * c, 64 * c + NV)), xo(c), A.subtract)
-
-    def race_v(c, nv=NV):
+    def race_v(c, nv):
         tt(t_("cmp", c, 0, 16 * nv), IND(EW, B("cu", 64 * c, 64 * c + nv)), t_("dv", c, 0, 16 * nv), A.is_gt)
+
+    def races_v(x, p, h):
+        cuts = [(c, j, min(j + h, NV)) for c in p for j in range(0, NV, h)]
+        for c, j0, j1 in cuts:
+            yield tt(t_("dv", c, 16 * j0, 16 * j1), IND(win(x, c), B("of", 64 * c + j0, 64 * c + j1)), xo(c, j0, j1), A.subtract)
+        for c, j0, j1 in cuts:
+            yield tt(t_("cmp", c, 16 * j0, 16 * j1), IND(EW, B("cu", 64 * c + j0, 64 * c + j1)), t_("dv", c, 16 * j0, 16 * j1), A.is_gt)
 
     def race_s(x, p, k, nv=NV):
         na = nv + 2 * ((66 - nv) // 4)
@@ -341,25 +347,31 @@ def rank_program(g, core, T, topo):
         yield ts(B("of", a, b - 1), oi, B("sv", 0, 1), A.add)
         yield cp(B("cu", a, b - 1), ca)
 
+    def masks(p, k):
+        a, b = 64 * p[0], 64 * p[-1] + 64
+        yield ts(B("sg", a, b), B(M(k + 1), a, b), 2.0 / HUGE, A.mult, -1.0, A.add)
+        if k == 0:
+            yield ts(UT(a, b), UT(a, b), 811.0, A.add)
+
     def later_intervals(x, day):
+        pa, pb = PARTS
         for k in range(2):
-            todo = [post(p, k, day) for p in PARTS]
-            for i, p in enumerate(PARTS):
-                a, b = 64 * p[0], 64 * p[-1] + 64
-                drain(todo[i])
-                rest = todo[i + 1] if i + 1 < len(PARTS) else iter(())
-                for c in p:
-                    race_v_diff(x, c)
-                    drain(rest, 1)
-                ts(B("sg", a, b), B(M(k + 1), a, b), 2.0 / HUGE, A.mult, -1.0, A.add)
-                for c in p:
-                    race_v(c)
-                    drain(rest, 1)
-                race_s(x, p, k + 1)
-                for c in p:
-                    counts(c, k + 1, day)
-                if k == 0:
-                    ts(UT(a, b), UT(a, b), 811.0, A.add)
+            drain(post(pa, k, day))
+            race_s(x, pa, k + 1)
+            lists, signs = post(pb, k, day), masks(pa, k)
+            for _ in races_v(x, pa, 16):
+                drain(lists, 1)
+            for c in pa:
+                counts(c, k + 1, day)
+            drain(lists, 1)
+            for _ in signs:
+                drain(lists, 1)
+            drain(lists)
+            race_s(x, pb, k + 1)
+            signs = masks(pb, k)
+            for _ in races_v(x, pb, NV):
+                drain(signs, 1)
+            counts(2, k + 1, day)
 
     TS, TW, TU = (6, 54), (0, 102), 3
     RS, RW, RU = (0, 60), (48, 54), 57
@@ -371,15 +383,15 @@ def rank_program(g, core, T, topo):
         cp(B("h1", 3, 6), ACC(63, 192, 64))
         ts(h2, h1, 13, SHR, 0x7F0, AND)
         ts(B("h3", 0, 3), B("h1", 0, 3), 8191, AND)
+        ts(B("hw", 0, 6), h1, 65535, AND)
+        ts(B("h4", 0, 3), B("h3", 0, 3), -4096.0, A.add, float(BETA), A.mult)
         for c in range(3):
             ts(B("hu", c, 6, 3), B("h2", c, 6, 3), B("sv", c, c + 1), A.add)
-        ts(B("hw", 0, 6), h1, 65535, AND)
-        cp(B(tx, 6, 102), IND(B(x, 0, 3 * CW), B("hu", 0, 6)))
-        ts(B("h1", 0, 3), B("h3", 0, 3), -4096.0, A.add, float(BETA), A.mult)
+        ts(B("h5", 0, 3), B("h4", 0, 3), 8191, AND)
         for i in range(2):
             cp(B(tx, TW[i], TW[i] + 3), B("hw", 3 * i, 3 * i + 3))
-        ts(B("h3", 0, 3), B("h1", 0, 3), 8191, AND)
-        ts(B(tx, TU, TU + 3), B("h3", 0, 3), float(4096 + 811 * (6 + day)), A.add)
+        cp(B(tx, 6, 102), IND(B(x, 0, 3 * CW), B("hu", 0, 6)))
+        ts(B(tx, TU, TU + 3), B("h5", 0, 3), float(4096 + 811 * (6 + day)), A.add)
 
     def send(day):
         tx, rx = "tx%d" % day, "rx%d" % day
@@ -414,17 +426,32 @@ def rank_program(g, core, T, topo):
             tt(B("q1", l, l + 3), u, w, A.add)
             if not day:
                 tt(B("q1", l + 3, l + 6), u if i else UT(1, 192, 64), B("wa", 0, 3) if i else w, A.add)
-        ts(B("q2", la, lb), B("q1", la, lb), 8191, AND)
+        if day:
+            for i in sides:
+                cp(B("p1", 3 * i, 3 * i + 3), B(rx, RW[i], RW[i] + 3))
         for i in sides:
             l = 48 * nb * i
             o, r = B(tx, TS[i], TS[i] + 48), B(rx, RS[i], RS[i] + 48)
             tt(B("mc", l, l + 48), o if i else r, r if i else o, A.subtract)
             if i == sides[0]:
-                cp(B("hu", 0, lb - la), B("q2", la, lb))
+                ts(B("q2", la, lb), B("q1", la, lb), 8191, AND)
             if not day:
                 e = B("xe", 48 * i, 48 * i + 48)
                 tt(B("mc", l + 48, l + 96), e if i else r, r if i else e, A.subtract)
+        a, b = 3 * sides[0], 3 * sides[-1] + 3
+        p1, p2, p3, p4 = (B(n, a, b) for n in ("p1", "p2", "p3", "p4"))
+        if day:
+            ts(p2, p1, 8191, AND)
+        cp(B("hu", 0, lb - la), B("q2", la, lb))
+        if day:
+            ts(p3, p1, 57344, AND)
+            ts(p4, p2, -4096.0, A.add, float(INV), A.mult)
         tt(B("mcmp", lo, hi), IND(EW, B("hu", 0, lb - la)), B("mc", lo, hi), A.is_gt)
+        if day:
+            ts(p2, p4, 8191, AND)
+            tt(B("pn", a, b), p2, p3, A.add)
+            for i in sides:
+                tt(B("nd", 3 * i, 3 * i + 3), B("pn", 3 * i, 3 * i + 3), B("yn", 189 * i, 189 * i + 3), A.subtract)
         u0, u1 = bank(), bank()
         mm(B(u0, lo, hi), B("blk", 0, 128), B("mcmp", lo, hi), True, True)
         for s in range(16):
@@ -445,40 +472,31 @@ def rank_program(g, core, T, topo):
         for i in sides:
             l = 48 * nb * i
             tt(B("mm", 48 * i, 48 * i + 48), B("mw", l, l + 48), B("mc", l, l + 48), A.mult)
-        for i in sides:
-            sub = A.subtract if i else A.add
-            if day:
-                tt(B("fin", 48 * i, 48 * i + 48), B(tx, TS[i], TS[i] + 48), B("mm", 48 * i, 48 * i + 48), sub)
-                continue
-            for c in range(3):
+        ts(B("nw", la, lb), B(u1, la, lb), 11.5 * C, A.is_gt)
+        news = [(c, i) for i in sides for c in range(3)]
+
+        def strengths(n):
+            for c, i in news[:n]:
                 a, b = TS[i] + 16 * c, 48 * i + 16 * c
-                tt(own("xb", c, 63 * i - 1, 63 * i), B(tx, a, a + 16), B("mm", b, b + 16), sub)
+                tt(own("xb", c, 63 * i - 1, 63 * i), B(tx, a, a + 16), B("mm", b, b + 16), A.subtract if i else A.add)
+            del news[:n]
         if day:
             for i in sides:
-                cp(B("p1", 3 * i, 3 * i + 3), B(rx, RW[i], RW[i] + 3))
-            a, b = 3 * sides[0], 3 * sides[-1] + 3
-            p1, p2, p3 = B("p1", a, b), B("p2", a, b), B("p3", a, b)
-            ts(p2, p1, 8191, AND)
-            ts(p3, p1, 57344, AND)
-            ts(p1, p2, -4096.0, A.add, float(INV), A.mult)
-            ts(B("nw", a, b), B(u1, a, b), 11.5 * C, A.is_gt)
-            ts(p2, p1, 8191, AND)
-            tt(B("pn", a, b), p2, p3, A.add)
-            for i in sides:
-                tt(B("nd", 3 * i, 3 * i + 3), B("pn", 3 * i, 3 * i + 3), B("yn", 189 * i, 189 * i + 3), A.subtract)
-            tt(B("nm", a, b), B("nw", a, b), B("nd", a, b), A.mult)
+                tt(B("fin", 48 * i, 48 * i + 48), B(tx, TS[i], TS[i] + 48), B("mm", 48 * i, 48 * i + 48), A.subtract if i else A.add)
+            tt(B("nm", la, lb), B("nw", la, lb), B("nd", la, lb), A.mult)
             for i in sides:
                 y = B("yn", 189 * i, 189 * i + 3)
                 tt(y, y, B("nm", 3 * i, 3 * i + 3), A.add)
             return
-        ts(B("nw", la, lb), B(u1, la, lb), 11.5 * C, A.is_gt)
         ts(B("zz", la, lb), B(u1, la, lb), -11.5 * C, A.add)
+        strengths(2)
         for i in sides:
-            z = B("z1", 62 * i + 1, 192, 64)
-            tt(B("dz", 3 * i, 3 * i + 3), B("zz", 6 * i + 3, 6 * i + 6), z, A.subtract)
+            tt(B("dz", 3 * i, 3 * i + 3), B("zz", 6 * i + 3, 6 * i + 6), B("z1", 62 * i + 1, 192, 64), A.subtract)
         for i in sides:
             tt(B("nm", 6 * i, 6 * i + 3), B("nw", 6 * i, 6 * i + 3), B("nd", 6 * i, 6 * i + 3), A.mult)
+            strengths(1)
             tt(B("zm", 3 * i, 3 * i + 3), B("nw", 6 * i, 6 * i + 3), B("dz", 3 * i, 3 * i + 3), A.mult)
+        strengths(9)
         for i in sides:
             z, y = B("z1", 62 * i + 1, 192, 64), Y(63 * i, 192, 64)
             tt(y, y, B("nm", 6 * i, 6 * i + 3), A.add)
@@ -491,7 +509,7 @@ def rank_program(g, core, T, topo):
             tt(UT(63, 192, 64), UT(63, 192, 64), B("nm", 9, 12), A.add)
 
     n1, n2, n3 = B("n1", 0, 192), B("n2", 0, 192), B("n3", 0, 192)
-    ni, wf, ut = B("ni", 0, 192), B("wf", 0, 192), UT(0, 192)
+    ni, so, wf, ut = B("ni", 0, 192), B("so", 0, 192), B("wf", 0, 192), UT(0, 192)
     for c in range(3):
         cp(B("n1", 64 * c, 64 * c + 64), B("bt", c, 192, 3))
     ts(n2, n1, 101.0, A.mult, 4096.0, A.add)
@@ -501,8 +519,8 @@ def rank_program(g, core, T, topo):
     tt(wf, ni, n3, A.add)
     ts(n3, n2, 8191, AND)
     cp(ut, n3)
-    first_list()
-    place_words()
+    drain(first_list())
+    drain(place_words())
     ts(ut, ut, 811.0, A.add)
     relay("s", 0, 0, 64)
     relay("v", 1, 0, 64)
@@ -524,30 +542,31 @@ def rank_program(g, core, T, topo):
     counts(2, 0, 0, NV0)
     later_intervals("xa", 0)
 
-    def source(a, b):
-        cp(B("ni", a, b), ACC(a, b))
-        ts(B("so", a, b), B("ni", a, b), 13, SHR, 0x7F0, AND)
-
-    def source_list(a, b):
-        source(a, b)
-        ts(B("su", a, b), B("so", a, b), B("sv", 0, 1), A.add)
     drain(post(PARTS[0], 2, 0))
-    source_list(0, 128)
+    cp(B("ni", 0, 128), ACC(0, 128))
+    ts(B("so", 0, 128), B("ni", 0, 128), 13, SHR, 0x7F0, AND)
+    ts(B("su", 0, 128), B("so", 0, 128), B("sv", 0, 1), A.add)
     perm("s", 0, 0, 64)
     perm("s", 1, 0, 64)
     drain(post(PARTS[1], 2, 0))
     heads_and_feet(0, "xa")
     send(0)
-    source_list(128, 192)
+    cp(B("ni", 128, 192), ACC(128, 192))
+    ts(B("so", 128, 192), B("ni", 128, 192), 13, SHR, 0x7F0, AND)
+    ts(n2, ni, 8191, AND)
+    ts(B("su", 128, 192), B("so", 128, 192), B("sv", 0, 1), A.add)
+    ts(n3, n2, -4096.0, A.add, float(BETA), A.mult)
     perm("s", 2, 32, 64)
     perm("v", 2, 0, 32)
 
-    ts(n2, ni, 8191, AND)
-    ts(wf, ni, 65535, AND)
-    ts(n3, n2, -4096.0, A.add, float(BETA), A.mult)
     ts(n2, n3, 8191, AND)
+    ts(wf, ni, 65535, AND)
     ts(ut, n2, float(4096 + 811 * 3), A.add)
-    first_list()
+    ts(B("wa", 0, 3), B("wf", 62, 192, 64), float((811 * (3 - 6)) % 8192), A.add)
+    words = place_words()
+    for _ in first_list():
+        drain(words, 1)
+    ts(B("uf", 0, 3), UT(63, 192, 64), float(811 * (6 - 3)), A.add)
     for c in range(3):
         first_diff("xb", c, NV1)
     for c in range(3):
@@ -559,9 +578,6 @@ def rank_program(g, core, T, topo):
         act(B("xe", 48 + 16 * c, 64 + 16 * c), own("xb", c, 61, 62))
     race_s("xb", (2,), 0, NV1)
     counts(1, 0, 1, NV1)
-    place_words()
-    ts(B("wa", 0, 3), B("wf", 62, 192, 64), float((811 * (3 - 6)) % 8192), A.add)
-    ts(B("uf", 0, 3), UT(63, 192, 64), float(811 * (6 - 3)), A.add)
     banks = meeting(0)
     counts(2, 0, 1, NV1)
     for c in range(3):
@@ -574,18 +590,18 @@ def rank_program(g, core, T, topo):
     drain(post(PARTS[1], 2, 1))
     heads_and_feet(1, "xb")
     send(1)
-    source(0, 192)
+    cp(ni, ACC(0, 192))
+    ts(so, ni, 13, SHR, 0x7F0, AND)
+    ts(n2, ni, 8191, AND)
     for c in range(3):
         ts(B("su", c, 192, 3), B("so", 64 * c, 64 * c + 64), B("sv", c, c + 1), A.add)
     first, end = (48 if up else 0), (3024 if down else 3072)
-    for q, a in (("s", 1024), ("s", 2048), ("v", 0)):
-        move(q, B("outb", a, a + 1024), IND(B("xb", 0, 3 * CW), B("su", a // 16, a // 16 + 64)))
-    dma("y", None, B("outb", 1024, 2048), "o1", out_ap=T.yx[:, 1024:2048])
-    dma("y", None, B("outb", first, 1024), "o2", out_ap=T.yx[:, first:1024])
-    dma("s", None, B("outb", 2048, end), "o6", out_ap=T.yx[:, 2048:end])
-    ts(n2, ni, 8191, AND)
-    ts(n3, ni, 57344, AND)
+    for e, q, sem, a, b in (("s", "y", "o1", 56, 124), ("v", "y", "o2", 0, 56), ("s", "s", "o6", 124, 192)):
+        move(e, B("outb", 16 * a, 16 * b), IND(B("xb", 0, 3 * CW), B("su", a, b)))
+        a, b = max(16 * a, first), min(16 * b, end)
+        dma(q, None, B("outb", a, b), sem, out_ap=T.yx[:, a:b])
     ts(n1, n2, -4096.0, A.add, float(INV), A.mult)
+    ts(n3, ni, 57344, AND)
     ts(n2, n1, 8191, AND)
     for c in range(3):
         tt(B("yn", c, 192, 3), B("n2", 64 * c, 64 * c + 64), B("n3", 64 * c, 64 * c + 64), A.add)

@@ -7,8 +7,11 @@ AND, SHR = A.bitwise_and, A.logical_shift_right
 C = float(2 ** 25)
 HUGE = float(2 ** 60)
 ONE = 131072.0
+UP = 128.0
 CW = 1040
-NV, NV0, NV1 = 28, 44, 44
+WRAP = 1632
+NV, NV0, NV1 = (36, 28, 28), (44, 44, 28), (36, 36, 44)
+OUT = (("v", "y", 0, 72), ("s", "y", 72, 132), ("s", "s", 132, 192))
 PARTS = ((0, 1), (2,))
 
 
@@ -22,8 +25,8 @@ BETA = centred(37 * INV)
 
 F, H, I, U = "float32", "bfloat16", "int32", "uint16"
 SCRATCH = {}
-for _n, _w, _t in (("xn", 3072, H), ("outb", 3072, H), ("ew", 8192, H), ("bt", 192, I), ("xa", 3 * CW, H), ("xb", 3 * CW, H), ("sel", 2048, H),
-                   ("jb0", 128, H), ("jb1", 128, H), ("jb", 128, H), ("one", 128, H), ("idp", 128, H), ("idn", 128, H), ("blk", 128, H),
+for _n, _w, _t in (("xn", 3072, H), ("outb", 3072, H), ("ew", 8192 + WRAP, H), ("bt", 192, I), ("xa", 3 * CW, H), ("xb", 3 * CW, H), ("sel", 2048, H),
+                   ("jb0", 128, H), ("jb1", 128, H), ("jb", 128, H), ("one", 128, H), ("idp", 128, H), ("idn", 128, H), ("blk", 128, H), ("blc", 128, H),
                    ("pi", 1, I), ("pj", 1, I), ("sv", 8, F), ("io48", 64, I), ("iob", 64, I),
                    ("pos", 192, F), ("zero", 192, F), ("rst", 192, F), ("neg", 192, H), ("rl", 192, U), ("n1", 192, I), ("n2", 192, I), ("n3", 192, I),
                    ("wf", 192, I), ("ni", 192, I), ("so", 192, I), ("su", 192, U), ("h1", 6, I), ("h2", 6, I), ("h3", 3, I), ("h4", 3, I), ("h5", 3, I),
@@ -31,20 +34,20 @@ for _n, _w, _t in (("xn", 3072, H), ("outb", 3072, H), ("ew", 8192, H), ("bt", 1
                    ("q1", 12, I), ("q2", 12, I), ("mc", 192, F), ("mm", 96, F), ("mcmp", 192, H), ("mw", 192, F), ("fin", 96, H), ("xe", 96, H),
                    ("wa", 3, F), ("uf", 3, F), ("nd", 12, F), ("nw", 12, F), ("nm", 12, F), ("zz", 12, F), ("dz", 6, F), ("zm", 6, F),
                    ("pn", 6, F), ("p1", 6, I), ("p2", 6, I), ("p3", 6, I), ("p4", 6, I), ("yn", 192, F),
-                   ("tx0", 108, F), ("tx1", 108, F), ("rx0", 108, F), ("rx1", 108, F), ("xo", 3 * 16 * NV, H),
+                   ("tx0", 108, F), ("tx1", 108, F), ("rx0", 108, F), ("rx1", 108, F), ("xo", 16 * sum(NV), H),
                    ("s", 192, F), ("xk", 192, F), ("t", 192, F), ("nk", 192, F), ("ys", 192, F), ("ra", 192, F), ("rb", 192, F), ("ma", 192, H), ("mb", 192, H),
-                   ("sg", 192, H), ("cs", 192, I), ("ca", 192, I), ("oi", 192, I), ("cu", 192, U), ("of", 192, U)):
+                   ("cs", 192, I), ("ca", 192, I), ("oi", 192, I), ("cu", 192, U), ("of", 192, U)):
     SCRATCH[_n] = ("sbuf", [128, _w], _t)
 for _c in range(3):
     for _n in ("dv", "cmp", "xr", "es"):
         SCRATCH["%s_%d" % (_n, _c)] = ("sbuf", [128, 1008], H)
-for _c in sorted(set((NV, NV0, NV1))):
+for _c in sorted(set(NV + NV0 + NV1)):
     SCRATCH["kc%d" % _c] = ("sbuf", [128, 64], H)
 PSUM = ("va", "vb", "z0", "z1", "u0", "u1", "u2", "u3")
 for _n in PSUM:
     SCRATCH[_n] = ("psum", [128, 512], F)
 QSEM = {"v": "qv", "s": "qs", "p": "qp", "g": "qg"}
-SEMAPHORES = ["qv", "qs", "qp", "qg", "db", "dx", "de", "o1", "o2", "o3", "o4", "o5", "o6", "rh0", "rf0", "rh1", "rf1", "loc"]
+SEMAPHORES = ["qv", "qs", "qp", "qg", "db", "dx", "de", "dw", "o1", "o3", "o4", "o5", "rh0", "rf0", "rh1", "rf1", "loc"]
 
 
 def B(name, a, b, step=1):
@@ -68,8 +71,9 @@ def win(x, c):
     return B(x, c * CW, (c + 1) * CW)
 
 
-def xo(c, j0=0, j1=NV):
-    return B("xo", 16 * (NV * c + j0), 16 * (NV * c + j1))
+def xo(c, j0=0, j1=None):
+    a = sum(NV[:c])
+    return B("xo", 16 * (a + j0), 16 * (a + (NV[c] if j1 is None else j1)))
 
 
 def Y(a, b, step=1):
@@ -96,12 +100,22 @@ def t_(n, c, a, b, step=1):
     return B("%s_%d" % (n, c), a, b, step)
 
 
+def zat(c):
+    return "z%d" % (c // 2), 64 * (c % 2)
+
+
 def drain(calls, n=99):
     for _ in zip(range(n), calls):
         pass
 
 
-EW = B("ew", 0, 8192)
+def chain(*sequences):
+    for x in sequences:
+        for y in x:
+            yield y
+
+
+EW, EWX = B("ew", 0, 8192), B("ew", 0, 8192 + WRAP)
 IDP, IDN = B("idp", 0, 128), B("idn", 0, 128)
 
 
@@ -196,6 +210,7 @@ def rank_program(g, core, T, topo):
     dma("y", B("bt", 0, 192), None, "db", in_ap=T.boat[:])
     dma("s", B("xn", 0, 3072), None, "dx", in_ap=T.x[:])
     dma("y", EW, None, "de", in_ap=T.enc[:])
+    dma("y", B("ew", 8192, 8192 + WRAP), None, "dw", in_ap=T.enc[:, 0:WRAP])
 
     gi(B("pi", 0, 1), [[0, 1]], 0, 1)
     gi(B("io48", 0, 64), [[48, 64]], 0, 0)
@@ -205,39 +220,38 @@ def rank_program(g, core, T, topo):
     gsel(B("jb1", 0, 128), B("jb0", 0, 128), [[-16, 8], [0, 16]], A.is_ge, -1.0, 0, 1)
     gsel(B("jb", 0, 128), B("jb1", 0, 128), [[16, 8], [0, 16]], A.is_ge, -1.0, 15, -1)
     gsel(IDP, B("one", 0, 128), [[-1, 128]], A.is_equal, 0.0, 0, 1)
-    for n, v in (("zero", 0.0), ("ra", 0.0), ("rb", 0.0), ("rst", 1.0), ("neg", -1.0)):
+    ts(B("pj", 0, 1), B("pi", 0, 1), 15, AND)
+    for c in range(3):
+        ts(B("sv", 4 + c, 5 + c), B("pj", 0, 1), float(16 * c), A.add)
+    for c in range(3):
+        ts(B("rl", 64 * c, 64 * c + 64), B("io48", 0, 64), B("sv", 4 + c, 5 + c), A.add)
+        ts(B("sv", c, c + 1), B("pj", 0, 1), float(CW * c), A.add)
+    for n, v in (("zero", 0.0), ("rst", 1.0), ("neg", -1.0)):
         fill(B(n, 0, 192), v)
     fill(B("rst", 0, 192, 64), 0.0)
+    for n in ("ra", "rb"):
+        fill(B(n, 0, 192, 128), 0.0)
     for c in range(3):
         fill(B("xa", c * CW, c * CW + 16), 512.0)
         fill(B("xb", c * CW, c * CW + 16), 512.0)
-    for n in sorted(set((NV, NV0, NV1))):
+    for n in sorted(set(NV + NV0 + NV1)):
         k = "kc%d" % n
         fill(B(k, 0, 64), -7.0 * C)
         fill(B(k, 1, 1 + n), -11.5 * C)
         fill(B(k, 0, 1), -float(2 ** 30))
+    ts(B("blc", 0, 128), B("jb", 0, 128), 0.0, A.is_ge, C, A.mult)
+    for s in range(16):
+        gsel(B("sel", 128 * s, 128 * s + 128), B("blc", 0, 128), [[0, 8], [1, 16]], A.is_equal, 0.0, -s, 0)
+    ts(B("blk", 0, 128), B("jb", 0, 128), 0.0, A.is_ge)
     fill(B("vb", 448, 449), 0.0)
-    fill(B("tx0", 105, 108), 0.0)
-    fill(B("tx1", 105, 108), 0.0)
-    ts(B("pj", 0, 1), B("pi", 0, 1), 15, AND)
-    for c in range(3):
-        ts(B("sv", c, c + 1), B("pj", 0, 1), float(CW * c), A.add)
-        ts(B("sv", 4 + c, 5 + c), B("pj", 0, 1), float(16 * c), A.add)
-    for c in range(3):
-        ts(B("rl", 64 * c, 64 * c + 64), B("io48", 0, 64), B("sv", 4 + c, 5 + c), A.add)
-        ts(B("pos", 64 * c, 64 * c + 64), B("iob", 0, 64), ONE, A.mult)
+    fill(B("tx0", 102, 105), 0.0)
+    fill(B("tx1", 102, 105), 0.0)
 
-    def move(q, dst, src):
-        if q == "v":
-            cp(dst, src)
-        else:
-            act(dst, src)
+    def relay(c):
+        act(own("xa", c, -1, 63), IND(B("xn", 0, 3072), B("rl", 64 * c, 64 * c + 64)), bias=UP)
 
-    def relay(q, c, b0, b1):
-        move(q, own("xa", c, b0 - 1, b1 - 1), IND(B("xn", 0, 3072), B("rl", 64 * c + b0, 64 * c + b1)))
-
-    def perm(q, c, b0, b1):
-        move(q, own("xb", c, b0 - 1, b1 - 1), IND(win("xa", c), B("su", 64 * c + b0, 64 * c + b1)))
+    def perm(c):
+        act(own("xb", c, -1, 63), IND(win("xa", c), B("su", 64 * c, 64 * c + 64)))
 
     def place_words():
         yield tt(Y(0, 192), B("wf", 0, 192), B("pos", 0, 192), A.add)
@@ -255,35 +269,31 @@ def rank_program(g, core, T, topo):
         return "u%d" % (turn[0] % 4)
 
     def first_diff(x, c, nv):
-        for j0 in range(0, nv, 32):
-            j1 = min(j0 + 32, nv)
-            o = B(bank(), 0, 16 * (j1 - j0))
-            mm(o, IDP, own(x, c, j0, j1, -1), True, False)
-            mm(o, IDN, own(x, c, j0, j1), False, True)
-            act(t_("dv", c, 16 * j0, 16 * j1), o)
+        scan(t_("dv", c, 0, 16 * nv), own(x, c, 0, nv, -1), own(x, c, 0, nv), 0.0, A.max, A.subtract)
 
     def race_v(c, nv):
         tt(t_("cmp", c, 0, 16 * nv), IND(EW, B("cu", 64 * c, 64 * c + nv)), t_("dv", c, 0, 16 * nv), A.is_gt)
 
     def races_v(x, p, h):
-        cuts = [(c, j, min(j + h, NV)) for c in p for j in range(0, NV, h)]
+        cuts = [(c, j, min(j + h, NV[c])) for c in p for j in range(0, NV[c], h)]
         for c, j0, j1 in cuts:
             yield tt(t_("dv", c, 16 * j0, 16 * j1), IND(win(x, c), B("of", 64 * c + j0, 64 * c + j1)), xo(c, j0, j1), A.subtract)
         for c, j0, j1 in cuts:
-            yield tt(t_("cmp", c, 16 * j0, 16 * j1), IND(EW, B("cu", 64 * c + j0, 64 * c + j1)), t_("dv", c, 16 * j0, 16 * j1), A.is_gt)
+            yield tt(t_("cmp", c, 16 * j0, 16 * j1), IND(EWX, B("cu", 64 * c + j0, 64 * c + j1)), t_("dv", c, 16 * j0, 16 * j1), A.is_gt)
 
-    def race_s(x, p, k, nv=NV):
-        na = nv + 2 * ((66 - nv) // 4)
+    def race_s(x, p, k, nvs=NV):
         signs = []
 
         def enc(c, u, j0, j1):
-            act(t_("es", c, 16 * j0, 16 * j1), IND(EW, B("cu", 64 * c + j0, 64 * c + j1)))
+            act(t_("es", c, 16 * j0, 16 * j1), IND(EWX if k else EW, B("cu", 64 * c + j0, 64 * c + j1)))
             mm(B(u, 0, 16 * (j1 - j0)), IDP, t_("es", c, 16 * j0, 16 * j1), False, True)
 
         def sign():
             for out, a in signs:
                 act(out, a, ACT.Sign, bias=-0.5)
         for c in p:
+            nv = nvs[c]
+            na = nv + 2 * ((66 - nv) // 4)
             halves = ((bank(), nv, na), (bank(), na, 63))
             if k:
                 act(t_("xr", c, 16 * nv, 1008), IND(win(x, c), B("of", 64 * c + nv, 64 * c + 63)))
@@ -301,26 +311,23 @@ def rank_program(g, core, T, topo):
             signs[:] = [(t_("cmp", c, 16 * j0, 16 * j1), B(u, 0, 16 * (j1 - j0))) for u, j0, j1 in halves]
         sign()
 
-    def zat(c, k, day):
-        return ("z1", 64 * c) if day and not k else ("z%d" % (c // 2), 64 * (c % 2))
-
-    def counts(c, k, day, nv=NV):
-        z, a = zat(c, k, day)
-        mm(B(z, a, a + 64), IDP, B("kc%d" % nv, 0, 64), True, False)
+    def counts(c, k, nvs=NV):
+        z, a = zat(c)
+        mm(B(z, a, a + 64), IDP, B("kc%d" % nvs[c], 0, 64), True, False)
         if k:
             mm(B(z, a + 1, a + 64), IDP, B(M(k), 64 * c + 1, 64 * c + 64), False, False)
         for s in range(16):
             mm(B(z, a + 1, a + 64), B("sel", 128 * s, 128 * s + 128), t_("cmp", c, s, 1008, 16), False, s == 15)
 
-    def post(p, k, day):
+    def post(p, k):
         last = k == 2
         a, b = 64 * p[0], 64 * p[-1] + 64
         n = b - a
-        zn, z = zat(p[0], k, day)
+        zn, z = zat(p[0])
         vt, vtr = B("vb", 192, 192 + n), B("vb", 192, 192 + n, -1)
         nbx, nbr = B("vb", 449 - n, 449), B("vb", 448 - n, 448, -1)
         s, t, x, nk, ys = (B(i, a, b) for i in ("s", "t", "xk", "nk", "ys"))
-        yield scan(s, B("sg" if k else "neg", a, b), B(zn, z, z + n), -1.0, A.mult, A.min)
+        yield scan(s, B("neg", a, b), B(zn, z, z + n), -1.0, A.mult, A.min)
         yield tt(vt, Y(a, b), s, A.min)
         yield scan(nbr, B(M(k) if k else "zero", a, b, -1), vtr, 0.0, A.min, A.max)
         yield tt(t, vt, B(R(k), a, b), A.min)
@@ -345,36 +352,28 @@ def rank_program(g, core, T, topo):
         yield ts(oi, cs, 13, SHR, 0x7F0, AND)
         yield ts(ca, cs, 8191, AND)
         yield ts(B("of", a, b - 1), oi, B("sv", 0, 1), A.add)
-        yield cp(B("cu", a, b - 1), ca)
+        yield ts(B("cu", a, b - 1), ca, float(811 * (k + 1)), A.add)
 
-    def masks(p, k):
-        a, b = 64 * p[0], 64 * p[-1] + 64
-        yield ts(B("sg", a, b), B(M(k + 1), a, b), 2.0 / HUGE, A.mult, -1.0, A.add)
-        if k == 0:
-            yield ts(UT(a, b), UT(a, b), 811.0, A.add)
-
-    def later_intervals(x, day):
+    def later_intervals(x, more=()):
         pa, pb = PARTS
+        more = iter(more)
         for k in range(2):
-            drain(post(pa, k, day))
+            for _ in post(pa, k):
+                drain(more, 1)
+            drain(more)
             race_s(x, pa, k + 1)
-            lists, signs = post(pb, k, day), masks(pa, k)
-            for _ in races_v(x, pa, 16):
+            lists = post(pb, k)
+            for _ in races_v(x, pa, 18):
                 drain(lists, 1)
             for c in pa:
-                counts(c, k + 1, day)
-            drain(lists, 1)
-            for _ in signs:
-                drain(lists, 1)
+                counts(c, k + 1)
             drain(lists)
             race_s(x, pb, k + 1)
-            signs = masks(pb, k)
-            for _ in races_v(x, pb, NV):
-                drain(signs, 1)
-            counts(2, k + 1, day)
+            drain(races_v(x, pb, 64))
+            counts(2, k + 1)
 
-    TS, TW, TU = (6, 54), (0, 102), 3
-    RS, RW, RU = (0, 60), (48, 54), 57
+    TS, TW, TU = (6, 54), (0, 105), 3
+    RS, RW, RU = (0, 60), (51, 54), 57
 
     def heads_and_feet(day, x):
         tx = "tx%d" % day
@@ -390,7 +389,11 @@ def rank_program(g, core, T, topo):
         ts(B("h5", 0, 3), B("h4", 0, 3), 8191, AND)
         for i in range(2):
             cp(B(tx, TW[i], TW[i] + 3), B("hw", 3 * i, 3 * i + 3))
-        cp(B(tx, 6, 102), IND(B(x, 0, 3 * CW), B("hu", 0, 6)))
+        src = IND(B(x, 0, 3 * CW), B("hu", 0, 6))
+        if day:
+            ts(B(tx, 6, 102), src, -UP, A.add)
+        else:
+            cp(B(tx, 6, 102), src)
         ts(B(tx, TU, TU + 3), B("h5", 0, 3), float(4096 + 811 * (6 + day)), A.add)
 
     def send(day):
@@ -414,102 +417,134 @@ def rank_program(g, core, T, topo):
 
     sides = [i for i, ok in ((0, up), (1, down)) if ok]
 
-    def meeting(day):
+    def at(i):
+        return 3 * sides.index(i)
+
+    def meeting(day, late=()):
         tx, rx = "tx%d" % day, "rx%d" % day
-        nb = 1 if day else 2
-        la, lb = 3 * nb * sides[0], 3 * nb * sides[-1] + 3 * nb
-        lo, hi = 16 * la, 16 * lb
+        n = 3 * len(sides)
+        lb = n if day else 2 * n
+        hi = 16 * lb
         for i in sides:
-            l = 3 * nb * i
+            l = at(i)
             u = B(rx, RU, RU + 3) if i else B(tx, TU, TU + 3)
             w = B(tx, TW[1], TW[1] + 3) if i else B(rx, RW[0], RW[0] + 3)
             tt(B("q1", l, l + 3), u, w, A.add)
             if not day:
-                tt(B("q1", l + 3, l + 6), u if i else UT(1, 192, 64), B("wa", 0, 3) if i else w, A.add)
+                tt(B("q1", n + l, n + l + 3), u if i else UT(1, 192, 64), B("wa", 0, 3) if i else w, A.add)
         if day:
-            for i in sides:
-                cp(B("p1", 3 * i, 3 * i + 3), B(rx, RW[i], RW[i] + 3))
+            cp(B("p1", 0, n), B(rx, RW[sides[0]], RW[sides[0]] + n))
         for i in sides:
-            l = 48 * nb * i
+            l = 16 * at(i)
             o, r = B(tx, TS[i], TS[i] + 48), B(rx, RS[i], RS[i] + 48)
             tt(B("mc", l, l + 48), o if i else r, r if i else o, A.subtract)
             if i == sides[0]:
-                ts(B("q2", la, lb), B("q1", la, lb), 8191, AND)
+                ts(B("q2", 0, lb), B("q1", 0, lb), 8191, AND)
             if not day:
                 e = B("xe", 48 * i, 48 * i + 48)
-                tt(B("mc", l + 48, l + 96), e if i else r, r if i else e, A.subtract)
-        a, b = 3 * sides[0], 3 * sides[-1] + 3
-        p1, p2, p3, p4 = (B(n, a, b) for n in ("p1", "p2", "p3", "p4"))
+                tt(B("mc", 16 * n + l, 16 * n + l + 48), e if i else r, r if i else e, A.subtract)
+        p1, p2, p3, p4 = (B(k, 0, n) for k in ("p1", "p2", "p3", "p4"))
         if day:
             ts(p2, p1, 8191, AND)
-        cp(B("hu", 0, lb - la), B("q2", la, lb))
+        cp(B("hu", 0, lb), B("q2", 0, lb))
         if day:
             ts(p3, p1, 57344, AND)
             ts(p4, p2, -4096.0, A.add, float(INV), A.mult)
-        tt(B("mcmp", lo, hi), IND(EW, B("hu", 0, lb - la)), B("mc", lo, hi), A.is_gt)
+        tt(B("mcmp", 0, hi), IND(EW, B("hu", 0, lb)), B("mc", 0, hi), A.is_gt)
         if day:
+            drain(late)
             ts(p2, p4, 8191, AND)
-            tt(B("pn", a, b), p2, p3, A.add)
+            tt(B("pn", 0, n), p2, p3, A.add)
             for i in sides:
-                tt(B("nd", 3 * i, 3 * i + 3), B("pn", 3 * i, 3 * i + 3), B("yn", 189 * i, 189 * i + 3), A.subtract)
+                tt(B("nd", at(i), at(i) + 3), B("pn", at(i), at(i) + 3), B("yn", 189 * i, 189 * i + 3), A.subtract)
         u0, u1 = bank(), bank()
-        mm(B(u0, lo, hi), B("blk", 0, 128), B("mcmp", lo, hi), True, True)
+        mm(B(u0, 0, 16 * n), B("blk", 0, 128), B("mcmp", 0, 16 * n), True, True)
         for s in range(16):
-            mm(B(u1, la, lb), B("sel", 128 * s, 128 * s + 128), B("mcmp", lo + s, hi, 16), s == 0, s == 15)
+            mm(B(u1, 0, lb), B("sel", 128 * s, 128 * s + 128), B("mcmp", s, hi, 16), s == 0, s == 15)
         return u0, u1
 
     def outcome(day, u0, u1):
         tx, rx = "tx%d" % day, "rx%d" % day
-        nb = 1 if day else 2
-        la, lb = 3 * nb * sides[0], 3 * nb * sides[-1] + 3 * nb
-        lo, hi = 16 * la, 16 * lb
+        n = 3 * len(sides)
         if not day:
-            for i in sides:
-                tt(B("nd", 6 * i, 6 * i + 3), B(rx, RW[i], RW[i] + 3), B(tx, TW[i], TW[i] + 3), A.subtract)
+            k = sides[0]
+            tt(B("nd", 0, n), B(rx, RW[k], RW[k] + n), B("hw", 3 * k, 3 * k + n), A.subtract)
             if down:
                 tt(B("nd", 9, 12), B(rx, RU, RU + 3), B("uf", 0, 3), A.subtract)
-        ts(B("mw", lo, hi), B(u0, lo, hi), 11.5, A.is_gt)
-        for i in sides:
-            l = 48 * nb * i
-            tt(B("mm", 48 * i, 48 * i + 48), B("mw", l, l + 48), B("mc", l, l + 48), A.mult)
-        ts(B("nw", la, lb), B(u1, la, lb), 11.5 * C, A.is_gt)
-        news = [(c, i) for i in sides for c in range(3)]
-
-        def strengths(n):
-            for c, i in news[:n]:
-                a, b = TS[i] + 16 * c, 48 * i + 16 * c
-                tt(own("xb", c, 63 * i - 1, 63 * i), B(tx, a, a + 16), B("mm", b, b + 16), A.subtract if i else A.add)
-            del news[:n]
+        ts(B("mw", 0, 16 * n), B(u0, 0, 16 * n), 11.5, A.is_gt)
+        ts(B("nw", 0, n), B(u1, 0, n), 11.5 * C, A.is_gt)
+        if not day:
+            ts(B("zz", 0, n), B(u1, n, 2 * n), -11.5 * C, A.add)
+        tt(B("mm", 0, 16 * n), B("mw", 0, 16 * n), B("mc", 0, 16 * n), A.mult)
         if day:
             for i in sides:
-                tt(B("fin", 48 * i, 48 * i + 48), B(tx, TS[i], TS[i] + 48), B("mm", 48 * i, 48 * i + 48), A.subtract if i else A.add)
-            tt(B("nm", la, lb), B("nw", la, lb), B("nd", la, lb), A.mult)
+                l = 16 * at(i)
+                tt(B("fin", 48 * i, 48 * i + 48), B(tx, TS[i], TS[i] + 48), B("mm", l, l + 48), A.subtract if i else A.add)
+            tt(B("nm", 0, n), B("nw", 0, n), B("nd", 0, n), A.mult)
             for i in sides:
                 y = B("yn", 189 * i, 189 * i + 3)
-                tt(y, y, B("nm", 3 * i, 3 * i + 3), A.add)
+                tt(y, y, B("nm", at(i), at(i) + 3), A.add)
             return
-        ts(B("zz", la, lb), B(u1, la, lb), -11.5 * C, A.add)
-        strengths(2)
-        for i in sides:
-            tt(B("dz", 3 * i, 3 * i + 3), B("zz", 6 * i + 3, 6 * i + 6), B("z1", 62 * i + 1, 192, 64), A.subtract)
-        for i in sides:
-            tt(B("nm", 6 * i, 6 * i + 3), B("nw", 6 * i, 6 * i + 3), B("nd", 6 * i, 6 * i + 3), A.mult)
-            strengths(1)
-            tt(B("zm", 3 * i, 3 * i + 3), B("nw", 6 * i, 6 * i + 3), B("dz", 3 * i, 3 * i + 3), A.mult)
-        strengths(9)
-        for i in sides:
-            z, y = B("z1", 62 * i + 1, 192, 64), Y(63 * i, 192, 64)
-            tt(y, y, B("nm", 6 * i, 6 * i + 3), A.add)
-            tt(z, z, B("zm", 3 * i, 3 * i + 3), A.add)
+        tt(B("nm", 0, n), B("nw", 0, n), B("nd", 0, n), A.mult)
         if down:
-            tt(B("nm", 9, 12), B("nw", 6, 9), B("nd", 9, 12), A.mult)
-        if up:
-            cp(B("ra", 1, 192, 64), Y(0, 192, 64))
+            tt(B("nm", 9, 12), B("nw", at(1), at(1) + 3), B("nd", 9, 12), A.mult)
+        for i in sides:
+            y = Y(63 * i, 192, 64)
+            tt(y, y, B("nm", at(i), at(i) + 3), A.add)
         if down:
             tt(UT(63, 192, 64), UT(63, 192, 64), B("nm", 9, 12), A.add)
+        if up:
+            cp(B("ra", 1, 192, 64), Y(0, 192, 64))
+
+        def strengths():
+            for c in range(3):
+                for i in sides:
+                    a, b = TS[i] + 16 * c, 16 * (at(i) + c)
+                    yield tt(own("xb", c, 63 * i - 1, 63 * i), B(tx, a, a + 16), B("mm", b, b + 16), A.subtract if i else A.add)
+
+        def held(p):
+            z, z0 = zat(p[0])
+            cols = [(at(i) + p[0], at(i) + p[-1] + 1, B(z, z0 + 62 * i + 1, z0 + 64 * len(p), 64)) for i in sides]
+            for a, b, v in cols:
+                yield tt(B("dz", a, b), B("zz", a, b), v, A.subtract)
+            for a, b, v in cols:
+                yield tt(B("zm", a, b), B("nw", a, b), B("dz", a, b), A.mult)
+            for a, b, v in cols:
+                yield tt(v, v, B("zm", a, b), A.add)
+        drain(held(PARTS[0]))
+        return chain(strengths(), held(PARTS[1]))
+
+    def decode(a, b):
+        n2, n3, ni = B("n2", a, b), B("n3", a, b), B("ni", a, b)
+        yield ts(n2, ni, 8191, AND)
+        yield ts(n3, n2, -4096.0, A.add, float(BETA), A.mult)
+        yield ts(B("wf", a, b), ni, 65535, AND)
+        yield ts(n2, n3, 8191, AND)
+        yield ts(UT(a, b), n2, float(4096 + 811 * 3), A.add)
+
+    def numbers(p):
+        a, b = 64 * p[0], 64 * p[-1] + 64
+        n1, n2, n3, ni = (B(n, a, b) for n in ("n1", "n2", "n3", "ni"))
+        yield ts(n2, ni, 8191, AND)
+        yield ts(n3, ni, 57344, AND)
+        yield ts(n1, n2, -4096.0, A.add, float(INV), A.mult)
+        yield
+        yield ts(n2, n1, 8191, AND)
+        yield
+        for c in p:
+            yield tt(B("yn", c, 192, 3), B("n2", 64 * c, 64 * c + 64), B("n3", 64 * c, 64 * c + 64), A.add)
+
+    def sources(p):
+        a, b = 64 * p[0], 64 * p[-1] + 64
+        yield cp(B("ni", a, b), ACC(a, b))
+        yield
+        yield ts(B("so", a, b), B("ni", a, b), 13, SHR, 0x7F0, AND)
+        yield
+        for c in p:
+            yield ts(B("su", c, 192, 3), B("so", 64 * c, 64 * c + 64), B("sv", c, c + 1), A.add)
 
     n1, n2, n3 = B("n1", 0, 192), B("n2", 0, 192), B("n3", 0, 192)
-    ni, so, wf, ut = B("ni", 0, 192), B("so", 0, 192), B("wf", 0, 192), UT(0, 192)
+    ni, wf, ut = B("ni", 0, 192), B("wf", 0, 192), UT(0, 192)
     for c in range(3):
         cp(B("n1", 64 * c, 64 * c + 64), B("bt", c, 192, 3))
     ts(n2, n1, 101.0, A.mult, 4096.0, A.add)
@@ -520,92 +555,86 @@ def rank_program(g, core, T, topo):
     ts(n3, n2, 8191, AND)
     cp(ut, n3)
     drain(first_list())
-    drain(place_words())
-    ts(ut, ut, 811.0, A.add)
-    relay("s", 0, 0, 64)
-    relay("v", 1, 0, 64)
-    relay("s", 2, 0, 32)
-    relay("v", 2, 32, 64)
+    for c in range(3):
+        relay(c)
+        ts(B("pos", 64 * c, 64 * c + 64), B("iob", 0, 64), ONE, A.mult)
     ts(IDN, IDP, -1.0, A.mult)
-    ts(B("blk", 0, 128), B("jb", 0, 128), 0.0, A.is_ge)
-    for s in range(16):
-        ts(B("sel", 128 * s, 128 * s + 128), B("jb", 0, 128), float(s), A.is_equal, C, A.mult)
     for c in range(3):
-        first_diff("xa", c, NV0)
-        cp(xo(c), own("xa", c, 0, NV))
+        first_diff("xa", c, NV0[c])
+    drain(place_words())
     for c in range(3):
-        race_v(c, NV0)
+        race_v(c, NV0[c])
+    for c in range(3):
+        cp(xo(c), own("xa", c, 0, NV[c]))
     race_s("xa", (0, 1), 0, NV0)
-    counts(0, 0, 0, NV0)
+    counts(0, 0, NV0)
+    counts(1, 0, NV0)
     race_s("xa", (2,), 0, NV0)
-    counts(1, 0, 0, NV0)
-    counts(2, 0, 0, NV0)
-    later_intervals("xa", 0)
+    counts(2, 0, NV0)
+    later_intervals("xa")
 
-    drain(post(PARTS[0], 2, 0))
+    drain(post(PARTS[0], 2))
     cp(B("ni", 0, 128), ACC(0, 128))
     ts(B("so", 0, 128), B("ni", 0, 128), 13, SHR, 0x7F0, AND)
     ts(B("su", 0, 128), B("so", 0, 128), B("sv", 0, 1), A.add)
-    perm("s", 0, 0, 64)
-    perm("s", 1, 0, 64)
-    drain(post(PARTS[1], 2, 0))
+    perm(0)
+    perm(1)
+    words = decode(0, 128)
+    for _ in post(PARTS[1], 2):
+        drain(words, 1)
     heads_and_feet(0, "xa")
     send(0)
     cp(B("ni", 128, 192), ACC(128, 192))
     ts(B("so", 128, 192), B("ni", 128, 192), 13, SHR, 0x7F0, AND)
-    ts(n2, ni, 8191, AND)
+    words = decode(128, 192)
+    drain(words, 1)
     ts(B("su", 128, 192), B("so", 128, 192), B("sv", 0, 1), A.add)
-    ts(n3, n2, -4096.0, A.add, float(BETA), A.mult)
-    perm("s", 2, 32, 64)
-    perm("v", 2, 0, 32)
+    drain(words, 1)
+    perm(2)
+    drain(words)
 
-    ts(n2, n3, 8191, AND)
-    ts(wf, ni, 65535, AND)
-    ts(ut, n2, float(4096 + 811 * 3), A.add)
     ts(B("wa", 0, 3), B("wf", 62, 192, 64), float((811 * (3 - 6)) % 8192), A.add)
     words = place_words()
     for _ in first_list():
         drain(words, 1)
     ts(B("uf", 0, 3), UT(63, 192, 64), float(811 * (6 - 3)), A.add)
     for c in range(3):
-        first_diff("xb", c, NV1)
-    for c in range(3):
-        race_v(c, NV1)
-    race_s("xb", (0, 1), 0, NV1)
-    counts(0, 0, 1, NV1)
+        first_diff("xb", c, NV1[c])
+    race_v(0, NV1[0])
+    race_v(1, NV1[1])
     for c in range(3):
         act(B("xe", 16 * c, 16 * c + 16), own("xb", c, 0, 1))
         act(B("xe", 48 + 16 * c, 64 + 16 * c), own("xb", c, 61, 62))
-    race_s("xb", (2,), 0, NV1)
-    counts(1, 0, 1, NV1)
+    race_s("xb", (0, 1), 0, NV1)
+    counts(0, 0, NV1)
     banks = meeting(0)
-    counts(2, 0, 1, NV1)
+    counts(1, 0, NV1)
+    race_s("xb", (2,), 0, NV1)
+    race_v(2, NV1[2])
+    counts(2, 0, NV1)
     for c in range(3):
-        act(xo(c), own("xb", c, 0, NV))
-    outcome(0, *banks)
-    ts(ut, ut, 811.0, A.add)
-    later_intervals("xb", 1)
+        act(xo(c), own("xb", c, 0, NV[c]))
+    later_intervals("xb", outcome(0, *banks))
 
-    drain(post(PARTS[0], 2, 1))
-    drain(post(PARTS[1], 2, 1))
+    drain(post(PARTS[0], 2))
+    ahead = chain(sources(PARTS[0]), numbers(PARTS[0]))
+    for _ in post(PARTS[1], 2):
+        drain(ahead, 1)
     heads_and_feet(1, "xb")
     send(1)
-    cp(ni, ACC(0, 192))
-    ts(so, ni, 13, SHR, 0x7F0, AND)
-    ts(n2, ni, 8191, AND)
-    for c in range(3):
-        ts(B("su", c, 192, 3), B("so", 64 * c, 64 * c + 64), B("sv", c, c + 1), A.add)
+    for _ in sources(PARTS[1]):
+        drain(ahead, 1)
     first, end = (48 if up else 0), (3024 if down else 3072)
-    for e, q, sem, a, b in (("s", "y", "o1", 56, 124), ("v", "y", "o2", 0, 56), ("s", "s", "o6", 124, 192)):
-        move(e, B("outb", 16 * a, 16 * b), IND(B("xb", 0, 3 * CW), B("su", a, b)))
+    for e, q, a, b in OUT:
+        dst, src = B("outb", 16 * a, 16 * b), IND(B("xb", 0, 3 * CW), B("su", a, b))
+        if e == "s":
+            act(dst, src, bias=-UP)
+        else:
+            ts(dst, src, -UP, A.add)
         a, b = max(16 * a, first), min(16 * b, end)
-        dma(q, None, B("outb", a, b), sem, out_ap=T.yx[:, a:b])
-    ts(n1, n2, -4096.0, A.add, float(INV), A.mult)
-    ts(n3, ni, 57344, AND)
-    ts(n2, n1, 8191, AND)
-    for c in range(3):
-        tt(B("yn", c, 192, 3), B("n2", 64 * c, 64 * c + 64), B("n3", 64 * c, 64 * c + 64), A.add)
-    outcome(1, *meeting(1))
+        dma(q, None, B("outb", a, b), "o1", out_ap=T.yx[:, a:b])
+    drain(ahead)
+    outcome(1, *meeting(1, numbers(PARTS[1])))
     if up:
         dma("s", None, B("fin", 0, 48), "o3", out_ap=T.yx[:, 0:48])
     if down:

from concourse.bass import DstId, RemoteDMATransfer
from concourse.mybir import AluOpType, ActivationFunctionType

A = AluOpType
ACT = ActivationFunctionType
AND, SHR = A.bitwise_and, A.logical_shift_right
C = float(2 ** 25)
HUGE = float(2 ** 60)
ONE = 131072.0
UP = 128.0
CW = 1040
WRAP = 1632
NV, NV0, NV1 = (36, 28, 28), (44, 44, 28), (36, 36, 44)
OUT = (("v", "y", 0, 72), ("s", "y", 72, 132), ("s", "s", 132, 192))
PARTS = ((0, 1), (2,))


def centred(v):
    v %= 8192
    return v - 8192 if v >= 4096 else v


INV = centred(pow(101, -1, 8192))
BETA = centred(37 * INV)

F, H, I, U = "float32", "bfloat16", "int32", "uint16"
SCRATCH = {}
for _n, _w, _t in (("xn", 3072, H), ("outb", 3072, H), ("ew", 8192 + WRAP, H), ("bt", 192, I), ("xa", 3 * CW, H), ("xb", 3 * CW, H), ("sel", 2048, H),
                   ("jb0", 128, H), ("jb1", 128, H), ("jb", 128, H), ("one", 128, H), ("idp", 128, H), ("idn", 128, H), ("blk", 128, H), ("blc", 128, H),
                   ("pi", 1, I), ("pj", 1, I), ("sv", 8, F), ("io48", 64, I), ("iob", 64, I),
                   ("pos", 192, F), ("zero", 192, F), ("rst", 192, F), ("neg", 192, H), ("rl", 192, U), ("n1", 192, I), ("n2", 192, I), ("n3", 192, I),
                   ("wf", 192, I), ("ni", 192, I), ("so", 192, I), ("su", 192, U), ("h1", 6, I), ("h2", 6, I), ("h3", 3, I), ("h4", 3, I), ("h5", 3, I),
                   ("hu", 12, U), ("hw", 6, I),
                   ("q1", 12, I), ("q2", 12, I), ("mc", 192, F), ("mm", 96, F), ("mcmp", 192, H), ("mw", 192, F), ("fin", 96, H), ("xe", 96, H),
                   ("wa", 3, F), ("uf", 3, F), ("nd", 12, F), ("nw", 12, F), ("nm", 12, F), ("zz", 12, F), ("dz", 6, F), ("zm", 6, F),
                   ("pn", 6, F), ("p1", 6, I), ("p2", 6, I), ("p3", 6, I), ("p4", 6, I), ("yn", 192, F),
                   ("tx0", 108, F), ("tx1", 108, F), ("rx0", 108, F), ("rx1", 108, F), ("xo", 16 * sum(NV), H),
                   ("s", 192, F), ("xk", 192, F), ("t", 192, F), ("nk", 192, F), ("ys", 192, F), ("ra", 192, F), ("rb", 192, F), ("ma", 192, H), ("mb", 192, H),
                   ("cs", 192, I), ("ca", 192, I), ("oi", 192, I), ("cu", 192, U), ("of", 192, U)):
    SCRATCH[_n] = ("sbuf", [128, _w], _t)
for _c in range(3):
    for _n in ("dv", "cmp", "xr", "es"):
        SCRATCH["%s_%d" % (_n, _c)] = ("sbuf", [128, 1008], H)
for _c in sorted(set(NV + NV0 + NV1)):
    SCRATCH["kc%d" % _c] = ("sbuf", [128, 64], H)
PSUM = ("va", "vb", "z0", "z1", "u0", "u1", "u2", "u3")
for _n in PSUM:
    SCRATCH[_n] = ("psum", [128, 512], F)
QSEM = {"v": "qv", "s": "qs", "p": "qp", "g": "qg"}
SEMAPHORES = ["qv", "qs", "qp", "qg", "db", "dx", "de", "dw", "o1", "o3", "o4", "o5", "rh0", "rf0", "rh1", "rf1", "loc"]


def B(name, a, b, step=1):
    return (name, a, b, step)


def IND(w, o):
    return ("ind", w, o)


def entries(v):
    return entries(v[1]) + entries(v[2]) if v[0] == "ind" else [v[:3]]


def own(x, c, j0, j1, shift=0):
    a = c * CW + 16 * (j0 + 2 + shift)
    return B(x, a, a + 16 * (j1 - j0))


def win(x, c):
    return B(x, c * CW, (c + 1) * CW)


def xo(c, j0=0, j1=None):
    a = sum(NV[:c])
    return B("xo", 16 * (a + j0), 16 * (a + (NV[c] if j1 is None else j1)))


def Y(a, b, step=1):
    return B("va", a, b, step)


def ACC(a, b, step=1):
    return B("va", 192 + a, 192 + b, step)


def UT(a, b, step=1):
    return B("vb", a, b, step)


def R(k):
    return "rb" if k % 2 else "ra"


def M(k):
    return "mb" if k % 2 else "ma"


def t_(n, c, a, b, step=1):
    return B("%s_%d" % (n, c), a, b, step)


def zat(c):
    return "z%d" % (c // 2), 64 * (c % 2)


def drain(calls, n=99):
    for _ in zip(range(n), calls):
        pass


def chain(*sequences):
    for x in sequences:
        for y in x:
            yield y


EW, EWX = B("ew", 0, 8192), B("ew", 0, 8192 + WRAP)
IDP, IDN = B("idp", 0, 128), B("idn", 0, 128)


def rank_program(g, core, T, topo):
    rank = T.rank_of(core)
    if rank is None:
        return
    n_ranks = len(T.cores)
    up, down = rank > 0, rank < n_ranks - 1
    queue = {"v": g.vector, "s": g.scalar, "p": g.tensor, "g": g, "y": g.sync}
    count = {}
    waited = {}
    log = {}

    def need(q, sem, val):
        if waited.get((q, sem), 0) < val:
            waited[(q, sem)] = val
            queue[q].wait_ge(T.sem[sem], val)

    def ap(v):
        if v[0] == "ind":
            return ap(v[1]).indirect(ap(v[2]))
        name, a, b, step = v
        if step == -1:
            return T[name][:, b - 1:(a - 1 if a > 0 else None):-1]
        return T[name][:, a:b] if step == 1 else T[name][:, a:b:step]

    def sync(q, reads, writes, sem, n):
        waits, new = {}, []
        for kind, views in (("r", reads), ("w", writes)):
            for v in views:
                for name, a, b in entries(v):
                    ps = name in PSUM
                    for k2, a2, b2, q2, s2, v2 in log.get(name, []):
                        if not ((ps and q2 != q) or (a < b2 and a2 < b and not (kind == "r" and k2 == "r"))):
                            continue
                        if q2 == q == "p":
                            continue
                        waits[s2] = max(waits.get(s2, 0), v2)
                    new.append((name, kind, a, b))
        for s2 in sorted(waits):
            need(q, s2, waits[s2])
        count[sem] = count.get(sem, 0) + n
        for name, kind, a, b in new:
            old = log.setdefault(name, [])
            if kind == "w":
                old[:] = [e for e in old if not (a <= e[1] and e[2] <= b and (name not in PSUM or e[3] == q))]
            else:
                old[:] = [e for e in old if not (e[0] == "r" and e[3] == q and a <= e[1] and e[2] <= b)]
            old.append((kind, a, b, q, sem, count[sem]))

    def op(q, reads, writes, call):
        sync(q, reads, writes, QSEM[q], 1)
        call().then_inc(T.sem[QSEM[q]], 1)

    def tt(out, a, b, o):
        op("v", [a, b], [out], lambda: g.vector.tensor_tensor(ap(out), ap(a), ap(b), o))

    def ts(out, a, s1, o1, s2=None, o2=None):
        rd = [a] + ([s1] if isinstance(s1, tuple) else [])
        p1 = ap(s1) if isinstance(s1, tuple) else s1
        if o2 is None:
            op("v", rd, [out], lambda: g.vector.tensor_scalar(ap(out), ap(a), p1, None, o1))
        else:
            op("v", rd, [out], lambda: g.vector.tensor_scalar(ap(out), ap(a), p1, s2, o1, o2))

    def cp(out, a):
        op("v", [a], [out], lambda: g.vector.tensor_copy(ap(out), ap(a)))

    def scan(out, d0, d1, init, o0, o1):
        op("v", [d0, d1], [out], lambda: g.vector.tensor_tensor_scan(ap(out), ap(d0), ap(d1), init, o0, o1))

    def fill(out, val):
        op("v", [], [out], lambda: g.vector.memset(ap(out), val))

    def act(out, a, func=ACT.Copy, **kw):
        op("s", [a], [out], lambda: g.scalar.activation(ap(out), ap(a), func, **kw))

    def mm(out, lhs, rhs, start, stop):
        op("p", [lhs, rhs], [out], lambda: g.tensor.matmul(ap(out), ap(lhs), ap(rhs), start, stop))

    def dma(q, out, a, sem, out_ap=None, in_ap=None):
        sync(q, [a] if a else [], [out] if out else [], sem, 16)
        queue[q].dma_start(ap(out) if out else out_ap, ap(a) if a else in_ap).then_inc(T.sem[sem], 16)

    def gi(out, pattern, base, cm, **kw):
        op("g", [], [out], lambda: g.iota(ap(out), pattern, base, cm, **kw))

    def gsel(out, a, pattern, cmpop, val, base, cm):
        op("g", [a], [out], lambda: g.affine_select(ap(out), ap(a), pattern, cmpop, val, base, cm))

    dma("y", B("bt", 0, 192), None, "db", in_ap=T.boat[:])
    dma("s", B("xn", 0, 3072), None, "dx", in_ap=T.x[:])
    dma("y", EW, None, "de", in_ap=T.enc[:])
    dma("y", B("ew", 8192, 8192 + WRAP), None, "dw", in_ap=T.enc[:, 0:WRAP])

    gi(B("pi", 0, 1), [[0, 1]], 0, 1)
    gi(B("io48", 0, 64), [[48, 64]], 0, 0)
    gi(B("iob", 0, 64), [[1, 64]], 1, 0)
    gi(B("jb0", 0, 128), [[0, 8], [1, 16]], 0, 0, allow_small_or_imprecise_dtypes=True)
    fill(B("one", 0, 128), 1.0)
    gsel(B("jb1", 0, 128), B("jb0", 0, 128), [[-16, 8], [0, 16]], A.is_ge, -1.0, 0, 1)
    gsel(B("jb", 0, 128), B("jb1", 0, 128), [[16, 8], [0, 16]], A.is_ge, -1.0, 15, -1)
    gsel(IDP, B("one", 0, 128), [[-1, 128]], A.is_equal, 0.0, 0, 1)
    ts(B("pj", 0, 1), B("pi", 0, 1), 15, AND)
    for c in range(3):
        ts(B("sv", 4 + c, 5 + c), B("pj", 0, 1), float(16 * c), A.add)
    for c in range(3):
        ts(B("rl", 64 * c, 64 * c + 64), B("io48", 0, 64), B("sv", 4 + c, 5 + c), A.add)
        ts(B("sv", c, c + 1), B("pj", 0, 1), float(CW * c), A.add)
    for n, v in (("zero", 0.0), ("rst", 1.0), ("neg", -1.0)):
        fill(B(n, 0, 192), v)
    fill(B("rst", 0, 192, 64), 0.0)
    for n in ("ra", "rb"):
        fill(B(n, 0, 192, 128), 0.0)
    for c in range(3):
        fill(B("xa", c * CW, c * CW + 16), 512.0)
        fill(B("xb", c * CW, c * CW + 16), 512.0)
    for n in sorted(set(NV + NV0 + NV1)):
        k = "kc%d" % n
        fill(B(k, 0, 64), -7.0 * C)
        fill(B(k, 1, 1 + n), -11.5 * C)
        fill(B(k, 0, 1), -float(2 ** 30))
    ts(B("blc", 0, 128), B("jb", 0, 128), 0.0, A.is_ge, C, A.mult)
    for s in range(16):
        gsel(B("sel", 128 * s, 128 * s + 128), B("blc", 0, 128), [[0, 8], [1, 16]], A.is_equal, 0.0, -s, 0)
    ts(B("blk", 0, 128), B("jb", 0, 128), 0.0, A.is_ge)
    fill(B("vb", 448, 449), 0.0)
    fill(B("tx0", 102, 105), 0.0)
    fill(B("tx1", 102, 105), 0.0)

    def relay(c):
        act(own("xa", c, -1, 63), IND(B("xn", 0, 3072), B("rl", 64 * c, 64 * c + 64)), bias=UP)

    def perm(c):
        act(own("xb", c, -1, 63), IND(win("xa", c), B("su", 64 * c, 64 * c + 64)))

    def place_words():
        yield tt(Y(0, 192), B("wf", 0, 192), B("pos", 0, 192), A.add)
        yield cp(B("ra", 1, 192), Y(0, 191))

    def first_list():
        yield tt(B("cs", 0, 191), UT(1, 192), B("wf", 0, 191), A.add)
        yield ts(B("ca", 0, 191), B("cs", 0, 191), 8191, AND)
        yield cp(B("cu", 0, 191), B("ca", 0, 191))

    turn = [0]

    def bank():
        turn[0] += 1
        return "u%d" % (turn[0] % 4)

    def first_diff(x, c, nv):
        scan(t_("dv", c, 0, 16 * nv), own(x, c, 0, nv, -1), own(x, c, 0, nv), 0.0, A.max, A.subtract)

    def race_v(c, nv):
        tt(t_("cmp", c, 0, 16 * nv), IND(EW, B("cu", 64 * c, 64 * c + nv)), t_("dv", c, 0, 16 * nv), A.is_gt)

    def races_v(x, p, h):
        cuts = [(c, j, min(j + h, NV[c])) for c in p for j in range(0, NV[c], h)]
        for c, j0, j1 in cuts:
            yield tt(t_("dv", c, 16 * j0, 16 * j1), IND(win(x, c), B("of", 64 * c + j0, 64 * c + j1)), xo(c, j0, j1), A.subtract)
        for c, j0, j1 in cuts:
            yield tt(t_("cmp", c, 16 * j0, 16 * j1), IND(EWX, B("cu", 64 * c + j0, 64 * c + j1)), t_("dv", c, 16 * j0, 16 * j1), A.is_gt)

    def race_s(x, p, k, nvs=NV):
        signs = []

        def enc(c, u, j0, j1):
            act(t_("es", c, 16 * j0, 16 * j1), IND(EWX if k else EW, B("cu", 64 * c + j0, 64 * c + j1)))
            mm(B(u, 0, 16 * (j1 - j0)), IDP, t_("es", c, 16 * j0, 16 * j1), False, True)

        def sign():
            for out, a in signs:
                act(out, a, ACT.Sign, bias=-0.5)
        for c in p:
            nv = nvs[c]
            na = nv + 2 * ((66 - nv) // 4)
            halves = ((bank(), nv, na), (bank(), na, 63))
            if k:
                act(t_("xr", c, 16 * nv, 1008), IND(win(x, c), B("of", 64 * c + nv, 64 * c + 63)))
            for i, (u, j0, j1) in enumerate(halves):
                o = B(u, 0, 16 * (j1 - j0))
                mm(o, IDP, own(x, c, j0, j1), True, False)
                mm(o, IDN, t_("xr", c, 16 * j0, 16 * j1) if k else own(x, c, j0, j1, -1), False, False)
                if not k:
                    enc(c, u, j0, j1)
                if i == (1 if k else 0):
                    sign()
            if k:
                for u, j0, j1 in halves:
                    enc(c, u, j0, j1)
            signs[:] = [(t_("cmp", c, 16 * j0, 16 * j1), B(u, 0, 16 * (j1 - j0))) for u, j0, j1 in halves]
        sign()

    def counts(c, k, nvs=NV):
        z, a = zat(c)
        mm(B(z, a, a + 64), IDP, B("kc%d" % nvs[c], 0, 64), True, False)
        if k:
            mm(B(z, a + 1, a + 64), IDP, B(M(k), 64 * c + 1, 64 * c + 64), False, False)
        for s in range(16):
            mm(B(z, a + 1, a + 64), B("sel", 128 * s, 128 * s + 128), t_("cmp", c, s, 1008, 16), False, s == 15)

    def post(p, k):
        last = k == 2
        a, b = 64 * p[0], 64 * p[-1] + 64
        n = b - a
        zn, z = zat(p[0])
        vt, vtr = B("vb", 192, 192 + n), B("vb", 192, 192 + n, -1)
        nbx, nbr = B("vb", 449 - n, 449), B("vb", 448 - n, 448, -1)
        s, t, x, nk, ys = (B(i, a, b) for i in ("s", "t", "xk", "nk", "ys"))
        yield scan(s, B("neg", a, b), B(zn, z, z + n), -1.0, A.mult, A.min)
        yield tt(vt, Y(a, b), s, A.min)
        yield scan(nbr, B(M(k) if k else "zero", a, b, -1), vtr, 0.0, A.min, A.max)
        yield tt(t, vt, B(R(k), a, b), A.min)
        yield tt(x, s, nbx, A.max)
        if k:
            yield tt(nk, nbx, B(M(k), a, b), A.subtract)
        else:
            yield tt(ACC(a, b), nbx, t, A.max)
        yield tt(ys if last else Y(a, b), Y(a, b), x, A.subtract)
        if k:
            yield tt(ACC(a, b), ACC(a, b), t, A.max)
        if not last:
            yield scan(B(R(k + 1), a + 1, b), B("rst", a, b - 1), Y(a, b - 1), 0.0, A.mult, A.max)
        if k:
            yield tt(ACC(a, b), ACC(a, b), nk, A.max)
        if last:
            yield tt(ACC(a, b), ACC(a, b), ys, A.max)
            return
        cs, oi, ca = B("cs", a, b - 1), B("oi", a, b - 1), B("ca", a, b - 1)
        yield tt(cs, UT(a + 1, b), B(R(k + 1), a + 1, b), A.add)
        yield ts(B(M(k + 1), a, b), Y(a, b), 0.0, A.is_le, HUGE, A.mult)
        yield ts(oi, cs, 13, SHR, 0x7F0, AND)
        yield ts(ca, cs, 8191, AND)
        yield ts(B("of", a, b - 1), oi, B("sv", 0, 1), A.add)
        yield ts(B("cu", a, b - 1), ca, float(811 * (k + 1)), A.add)

    def later_intervals(x, more=()):
        pa, pb = PARTS
        more = iter(more)
        for k in range(2):
            for _ in post(pa, k):
                drain(more, 1)
            drain(more)
            race_s(x, pa, k + 1)
            lists = post(pb, k)
            for _ in races_v(x, pa, 18):
                drain(lists, 1)
            for c in pa:
                counts(c, k + 1)
            drain(lists)
            race_s(x, pb, k + 1)
            drain(races_v(x, pb, 64))
            counts(2, k + 1)

    TS, TW, TU = (6, 54), (0, 105), 3
    RS, RW, RU = (0, 60), (51, 54), 57

    def heads_and_feet(day, x):
        tx = "tx%d" % day
        h1, h2 = B("h1", 0, 6), B("h2", 0, 6)
        cp(B("h1", 0, 3), ACC(0, 192, 64))
        cp(B("h1", 3, 6), ACC(63, 192, 64))
        ts(h2, h1, 13, SHR, 0x7F0, AND)
        ts(B("h3", 0, 3), B("h1", 0, 3), 8191, AND)
        ts(B("hw", 0, 6), h1, 65535, AND)
        ts(B("h4", 0, 3), B("h3", 0, 3), -4096.0, A.add, float(BETA), A.mult)
        for c in range(3):
            ts(B("hu", c, 6, 3), B("h2", c, 6, 3), B("sv", c, c + 1), A.add)
        ts(B("h5", 0, 3), B("h4", 0, 3), 8191, AND)
        for i in range(2):
            cp(B(tx, TW[i], TW[i] + 3), B("hw", 3 * i, 3 * i + 3))
        src = IND(B(x, 0, 3 * CW), B("hu", 0, 6))
        if day:
            ts(B(tx, 6, 102), src, -UP, A.add)
        else:
            cp(B(tx, 6, 102), src)
        ts(B(tx, TU, TU + 3), B("h5", 0, 3), float(4096 + 811 * (6 + day)), A.add)

    def send(day):
        tx, rx = "tx%d" % day, "rx%d" % day
        calls = ([(rank - 1, 0, 54, "rh%d" % day)] if up else []) + ([(rank + 1, 54, 0, "rf%d" % day)] if down else [])
        sync("g", [B(tx, 0, 108)], [], "loc", 0)
        trs = []
        for i, (r, a, b, sem) in enumerate(calls):
            es = topo.engines(core, T.cores[r])
            es = es[i * len(es) // len(calls):(i + 1) * len(es) // len(calls)]
            rid, pid, _ = topo.addr(T.cores[r])
            trs.append(RemoteDMATransfer(dst_ids=[DstId(rid=rid, pnc=pid)], dma_engine_mask=sum(1 << e for e in es), remote_sem=T.sem[sem],
                                         src=T[tx][:, a:a + 54], dst=T[rx][:, b:b + 54]))
            count["loc"] = count.get("loc", 0) + len(es)
        g.remote_dma_fused(trs, local_sem=T.sem["loc"])
        for ok, r, a, sem in ((up, rank - 1, 0, "rf%d" % day), (down, rank + 1, 54, "rh%d" % day)):
            if ok:
                fan = (1 if r > 0 else 0) + (1 if r < n_ranks - 1 else 0)
                count[sem] = len(topo.engines(T.cores[r], core)) // fan
                log.setdefault(rx, []).append(("w", a, a + 54, "remote", sem, count[sem]))

    sides = [i for i, ok in ((0, up), (1, down)) if ok]

    def at(i):
        return 3 * sides.index(i)

    def meeting(day, late=()):
        tx, rx = "tx%d" % day, "rx%d" % day
        n = 3 * len(sides)
        lb = n if day else 2 * n
        hi = 16 * lb
        for i in sides:
            l = at(i)
            u = B(rx, RU, RU + 3) if i else B(tx, TU, TU + 3)
            w = B(tx, TW[1], TW[1] + 3) if i else B(rx, RW[0], RW[0] + 3)
            tt(B("q1", l, l + 3), u, w, A.add)
            if not day:
                tt(B("q1", n + l, n + l + 3), u if i else UT(1, 192, 64), B("wa", 0, 3) if i else w, A.add)
        if day:
            cp(B("p1", 0, n), B(rx, RW[sides[0]], RW[sides[0]] + n))
        for i in sides:
            l = 16 * at(i)
            o, r = B(tx, TS[i], TS[i] + 48), B(rx, RS[i], RS[i] + 48)
            tt(B("mc", l, l + 48), o if i else r, r if i else o, A.subtract)
            if i == sides[0]:
                ts(B("q2", 0, lb), B("q1", 0, lb), 8191, AND)
            if not day:
                e = B("xe", 48 * i, 48 * i + 48)
                tt(B("mc", 16 * n + l, 16 * n + l + 48), e if i else r, r if i else e, A.subtract)
        p1, p2, p3, p4 = (B(k, 0, n) for k in ("p1", "p2", "p3", "p4"))
        if day:
            ts(p2, p1, 8191, AND)
        cp(B("hu", 0, lb), B("q2", 0, lb))
        if day:
            ts(p3, p1, 57344, AND)
            ts(p4, p2, -4096.0, A.add, float(INV), A.mult)
        tt(B("mcmp", 0, hi), IND(EW, B("hu", 0, lb)), B("mc", 0, hi), A.is_gt)
        if day:
            drain(late)
            ts(p2, p4, 8191, AND)
            tt(B("pn", 0, n), p2, p3, A.add)
            for i in sides:
                tt(B("nd", at(i), at(i) + 3), B("pn", at(i), at(i) + 3), B("yn", 189 * i, 189 * i + 3), A.subtract)
        u0, u1 = bank(), bank()
        mm(B(u0, 0, 16 * n), B("blk", 0, 128), B("mcmp", 0, 16 * n), True, True)
        for s in range(16):
            mm(B(u1, 0, lb), B("sel", 128 * s, 128 * s + 128), B("mcmp", s, hi, 16), s == 0, s == 15)
        return u0, u1

    def outcome(day, u0, u1):
        tx, rx = "tx%d" % day, "rx%d" % day
        n = 3 * len(sides)
        if not day:
            k = sides[0]
            tt(B("nd", 0, n), B(rx, RW[k], RW[k] + n), B("hw", 3 * k, 3 * k + n), A.subtract)
            if down:
                tt(B("nd", 9, 12), B(rx, RU, RU + 3), B("uf", 0, 3), A.subtract)
        ts(B("mw", 0, 16 * n), B(u0, 0, 16 * n), 11.5, A.is_gt)
        ts(B("nw", 0, n), B(u1, 0, n), 11.5 * C, A.is_gt)
        if not day:
            ts(B("zz", 0, n), B(u1, n, 2 * n), -11.5 * C, A.add)
        tt(B("mm", 0, 16 * n), B("mw", 0, 16 * n), B("mc", 0, 16 * n), A.mult)
        if day:
            for i in sides:
                l = 16 * at(i)
                tt(B("fin", 48 * i, 48 * i + 48), B(tx, TS[i], TS[i] + 48), B("mm", l, l + 48), A.subtract if i else A.add)
            tt(B("nm", 0, n), B("nw", 0, n), B("nd", 0, n), A.mult)
            for i in sides:
                y = B("yn", 189 * i, 189 * i + 3)
                tt(y, y, B("nm", at(i), at(i) + 3), A.add)
            return
        tt(B("nm", 0, n), B("nw", 0, n), B("nd", 0, n), A.mult)
        if down:
            tt(B("nm", 9, 12), B("nw", at(1), at(1) + 3), B("nd", 9, 12), A.mult)
        for i in sides:
            y = Y(63 * i, 192, 64)
            tt(y, y, B("nm", at(i), at(i) + 3), A.add)
        if down:
            tt(UT(63, 192, 64), UT(63, 192, 64), B("nm", 9, 12), A.add)
        if up:
            cp(B("ra", 1, 192, 64), Y(0, 192, 64))

        def strengths():
            for c in range(3):
                for i in sides:
                    a, b = TS[i] + 16 * c, 16 * (at(i) + c)
                    yield tt(own("xb", c, 63 * i - 1, 63 * i), B(tx, a, a + 16), B("mm", b, b + 16), A.subtract if i else A.add)

        def held(p):
            z, z0 = zat(p[0])
            cols = [(at(i) + p[0], at(i) + p[-1] + 1, B(z, z0 + 62 * i + 1, z0 + 64 * len(p), 64)) for i in sides]
            for a, b, v in cols:
                yield tt(B("dz", a, b), B("zz", a, b), v, A.subtract)
            for a, b, v in cols:
                yield tt(B("zm", a, b), B("nw", a, b), B("dz", a, b), A.mult)
            for a, b, v in cols:
                yield tt(v, v, B("zm", a, b), A.add)
        drain(held(PARTS[0]))
        return chain(strengths(), held(PARTS[1]))

    def decode(a, b):
        n2, n3, ni = B("n2", a, b), B("n3", a, b), B("ni", a, b)
        yield ts(n2, ni, 8191, AND)
        yield ts(n3, n2, -4096.0, A.add, float(BETA), A.mult)
        yield ts(B("wf", a, b), ni, 65535, AND)
        yield ts(n2, n3, 8191, AND)
        yield ts(UT(a, b), n2, float(4096 + 811 * 3), A.add)

    def numbers(p):
        a, b = 64 * p[0], 64 * p[-1] + 64
        n1, n2, n3, ni = (B(n, a, b) for n in ("n1", "n2", "n3", "ni"))
        yield ts(n2, ni, 8191, AND)
        yield ts(n3, ni, 57344, AND)
        yield ts(n1, n2, -4096.0, A.add, float(INV), A.mult)
        yield
        yield ts(n2, n1, 8191, AND)
        yield
        for c in p:
            yield tt(B("yn", c, 192, 3), B("n2", 64 * c, 64 * c + 64), B("n3", 64 * c, 64 * c + 64), A.add)

    def sources(p):
        a, b = 64 * p[0], 64 * p[-1] + 64
        yield cp(B("ni", a, b), ACC(a, b))
        yield
        yield ts(B("so", a, b), B("ni", a, b), 13, SHR, 0x7F0, AND)
        yield
        for c in p:
            yield ts(B("su", c, 192, 3), B("so", 64 * c, 64 * c + 64), B("sv", c, c + 1), A.add)

    n1, n2, n3 = B("n1", 0, 192), B("n2", 0, 192), B("n3", 0, 192)
    ni, wf, ut = B("ni", 0, 192), B("wf", 0, 192), UT(0, 192)
    for c in range(3):
        cp(B("n1", 64 * c, 64 * c + 64), B("bt", c, 192, 3))
    ts(n2, n1, 101.0, A.mult, 4096.0, A.add)
    ts(n3, n1, 57344, AND)
    ts(ni, n2, 8191, AND)
    ts(n2, n1, 37.0, A.mult, 4096.0, A.add)
    tt(wf, ni, n3, A.add)
    ts(n3, n2, 8191, AND)
    cp(ut, n3)
    drain(first_list())
    for c in range(3):
        relay(c)
        ts(B("pos", 64 * c, 64 * c + 64), B("iob", 0, 64), ONE, A.mult)
    ts(IDN, IDP, -1.0, A.mult)
    for c in range(3):
        first_diff("xa", c, NV0[c])
    drain(place_words())
    for c in range(3):
        race_v(c, NV0[c])
    for c in range(3):
        cp(xo(c), own("xa", c, 0, NV[c]))
    race_s("xa", (0, 1), 0, NV0)
    counts(0, 0, NV0)
    counts(1, 0, NV0)
    race_s("xa", (2,), 0, NV0)
    counts(2, 0, NV0)
    later_intervals("xa")

    drain(post(PARTS[0], 2))
    cp(B("ni", 0, 128), ACC(0, 128))
    ts(B("so", 0, 128), B("ni", 0, 128), 13, SHR, 0x7F0, AND)
    ts(B("su", 0, 128), B("so", 0, 128), B("sv", 0, 1), A.add)
    perm(0)
    perm(1)
    words = decode(0, 128)
    for _ in post(PARTS[1], 2):
        drain(words, 1)
    heads_and_feet(0, "xa")
    send(0)
    cp(B("ni", 128, 192), ACC(128, 192))
    ts(B("so", 128, 192), B("ni", 128, 192), 13, SHR, 0x7F0, AND)
    words = decode(128, 192)
    drain(words, 1)
    ts(B("su", 128, 192), B("so", 128, 192), B("sv", 0, 1), A.add)
    drain(words, 1)
    perm(2)
    drain(words)

    ts(B("wa", 0, 3), B("wf", 62, 192, 64), float((811 * (3 - 6)) % 8192), A.add)
    words = place_words()
    for _ in first_list():
        drain(words, 1)
    ts(B("uf", 0, 3), UT(63, 192, 64), float(811 * (6 - 3)), A.add)
    for c in range(3):
        first_diff("xb", c, NV1[c])
    race_v(0, NV1[0])
    race_v(1, NV1[1])
    for c in range(3):
        act(B("xe", 16 * c, 16 * c + 16), own("xb", c, 0, 1))
        act(B("xe", 48 + 16 * c, 64 + 16 * c), own("xb", c, 61, 62))
    race_s("xb", (0, 1), 0, NV1)
    counts(0, 0, NV1)
    banks = meeting(0)
    counts(1, 0, NV1)
    race_s("xb", (2,), 0, NV1)
    race_v(2, NV1[2])
    counts(2, 0, NV1)
    for c in range(3):
        act(xo(c), own("xb", c, 0, NV[c]))
    later_intervals("xb", outcome(0, *banks))

    drain(post(PARTS[0], 2))
    ahead = chain(sources(PARTS[0]), numbers(PARTS[0]))
    for _ in post(PARTS[1], 2):
        drain(ahead, 1)
    heads_and_feet(1, "xb")
    send(1)
    for _ in sources(PARTS[1]):
        drain(ahead, 1)
    first, end = (48 if up else 0), (3024 if down else 3072)
    for e, q, a, b in OUT:
        dst, src = B("outb", 16 * a, 16 * b), IND(B("xb", 0, 3 * CW), B("su", a, b))
        if e == "s":
            act(dst, src, bias=-UP)
        else:
            ts(dst, src, -UP, A.add)
        a, b = max(16 * a, first), min(16 * b, end)
        dma(q, None, B("outb", a, b), "o1", out_ap=T.yx[:, a:b])
    drain(ahead)
    outcome(1, *meeting(1, numbers(PARTS[1])))
    if up:
        dma("s", None, B("fin", 0, 48), "o3", out_ap=T.yx[:, 0:48])
    if down:
        dma("y", None, B("fin", 48, 96), "o4", out_ap=T.yx[:, 3024:3072])
    dma("y" if up else "s", None, B("yn", 0, 192), "o5", out_ap=T.yb[:])
    for sem in sorted(count):
        if count[sem]:
            need("g", sem, count[sem])
